import numpy as np
import ml_dtypes


def mxq(x, axis, fmt="e4m3"):
    dtype, down = {"e4m3": (ml_dtypes.float8_e4m3fn, 7), "e5m2": (ml_dtypes.float8_e5m2, 14)}[fmt]
    v = np.moveaxis(np.asarray(x, np.float32).astype(ml_dtypes.bfloat16).astype(np.float64), axis, -1)
    blocks = v.reshape(v.shape[:-1] + (-1, 32))
    amax = np.abs(blocks).max(-1, keepdims=True)
    byte = np.maximum(np.where(amax > 0, np.frexp(amax)[1] - 1 + 127, 0) - down, 1)
    scale = np.exp2(byte - 127.0)
    codes = (blocks / scale).astype(np.float32).astype(dtype).astype(np.float64)
    return np.moveaxis((codes * scale).reshape(v.shape), -1, axis)


WIDE = False


def mx_kscale(k):
    if not WIDE:
        return np.ones(k)
    levels = np.array([10, -10, 5, -5, 0])
    if k % 512:
        return np.exp2(np.random.permutation(np.resize(levels, k // 32))).repeat(32)
    a = np.empty((k // 512, 16))
    for p in range(k // 512):
        a[p, :8] = np.random.permutation(np.resize(levels, 8))
        for g in range(8):
            far = levels[np.abs(levels - a[p, g]) >= 10]
            a[p, g + 8] = far[np.random.randint(len(far))]
    return np.exp2(a.ravel()).repeat(32)


def f64(x):
    return np.asarray(x).astype(np.float64)


def striped(idx):
    return np.tile(idx.reshape(-1, 16).T, (8, 1)).astype(np.uint16)


def unstriped(offs):
    return offs[:16].T.reshape(-1).astype(np.int64)


E2M1 = np.array([0.0, 0.5, 1.0, 1.5, 2.0, 3.0, 4.0, 6.0, -0.0, -0.5, -1.0, -1.5, -2.0, -3.0, -4.0, -6.0])


def pack_weight(w, fmt):
    k, n = w.shape
    w = f64(np.asarray(w, np.float32).astype(ml_dtypes.bfloat16)).reshape(k // 32, 32, n)
    amax = np.abs(w).max(1)
    if fmt == "e4m3":
        byte = np.frexp(amax)[1] - 1 + 127 - 7
    else:
        mant, ex = np.frexp(amax / 6.0)
        byte = np.where(mant > 0.5, ex, ex - 1) + 127
    byte = np.clip(np.where(amax > 0, byte, 1), 1, 254)
    scaled = (w * np.exp2(127.0 - byte)[:, None, :]).reshape(k, n).astype(np.float32)
    by_word = np.ascontiguousarray(scaled.reshape(k // 512, 128, 4, n).transpose(0, 1, 3, 2))
    if fmt == "e4m3":
        words = by_word.astype(ml_dtypes.float8_e4m3fn).view(np.uint8)
    else:
        c = by_word.astype(ml_dtypes.float4_e2m1fn).view(np.uint8) & 0xF
        words = (c[..., 0::2] | (c[..., 1::2] << 4)).reshape(k // 512, 128, 2 * n)
    return np.ascontiguousarray(words), np.ascontiguousarray(byte.astype(np.uint8).reshape(k // 512, 16, n))


def unpack_weight(words, scales, fmt):
    g, _, n = scales.shape
    words = np.ascontiguousarray(words).reshape(g, 128, n, -1)
    if fmt == "e4m3":
        vals = words.view(ml_dtypes.float8_e4m3fn).astype(np.float64)
    else:
        nib = np.empty((g, 128, n, 4), np.uint8)
        nib[..., 0::2] = words & 0xF
        nib[..., 1::2] = words >> 4
        vals = E2M1[nib]
    vals = vals * np.repeat(np.exp2(scales.astype(np.float64) - 127.0), 8, axis=1)[..., None]
    return vals.transpose(0, 1, 3, 2).reshape(g * 512, n)


def gelu(v):
    return 0.5 * v * (1.0 + np.tanh(np.sqrt(2.0 / np.pi) * (v + 0.044715 * v**3)))


K, H, N, T, S, T2, P = 1024, 1024, 384, 2048, 1024, 2048, 1024

def setup_inputs():
    n = np.random.standard_normal
    s = mx_kscale(K)[:, None]
    u = mx_kscale(H)[:, None]
    tab_words, tab_scales = pack_weight(n((K, T)) * s, "e4m3")
    w4_words, w4_scales = pack_weight(n((H, N)) / np.sqrt(H) / u, "e2m1")
    return {
        "tab_words": tab_words, "tab_scales": tab_scales,
        "offs": striped(np.random.permutation(T)[:S]),
        "offs2": striped(np.random.permutation(T2)[:S]),
        "offs3": striped(np.random.permutation(T2)[:P]),
        "offs4": striped(np.random.permutation(T2)[:P]),
        "w1": (1.5 * n((K, H)) / np.sqrt(K) / s).astype(np.float32),
        "wgs": np.exp(0.3 * n((128, S))).astype(np.float32),
        "rate": (np.exp(0.5 * n((H, P))) * u).astype(np.float32),
        "w4_words": w4_words, "w4_scales": w4_scales,
    }

def reference(tab_words, tab_scales, offs, offs2, offs3, offs4, w1, wgs, rate, w4_words, w4_scales):
    v = unpack_weight(tab_words, tab_scales, "e4m3")[:, unstriped(offs)]
    a = mxq(f64(w1), 0, "e4m3").T @ v
    h = a / (1.0 + np.exp(-a))
    page = np.zeros((H, T2))
    page[:, unstriped(offs2)] = np.tile(f64(wgs), (H // 128, 1)) * h
    x1 = page[:, unstriped(offs3)]
    x2 = page[:, unstriped(offs4)]
    d = x1 - x2
    z = f64(rate) * (1.0 / (1.0 + d * d))
    w4 = unpack_weight(w4_words, w4_scales, "e2m1")
    return w4.T @ mxq(z, 0, "e4m3")

@@ -1,0 +1,250 @@
+from contextlib import ExitStack
+
+import concourse.mybir as mybir
+
+K, H, N, T, S, T2, HOPS = 1024, 1024, 384, 2048, 1024, 2048, 1024
+FLOPS = 2 * K * H * S + 2 * H * N * HOPS
+
+F32 = mybir.dt.float32
+BF16 = mybir.dt.bfloat16
+I32 = mybir.dt.int32
+U32 = mybir.dt.uint32
+U16 = mybir.dt.uint16
+U8 = mybir.dt.uint8
+FP8X4 = mybir.dt.float8_e4m3fn_x4
+FP4X4 = mybir.dt.float4_e2m1fn_x4
+ACT = mybir.ActivationFunctionType
+ALU = mybir.AluOpType
+
+P = 128
+PACK = 4
+KP = P * PACK
+PASSES = 2
+HALF = 512
+CHUNK = 256
+SUB = 128
+NT = N // P
+
+
+def tile_list_vacancy_hop_barriers_kernel(
+    tc, tab_words, tab_scales, offs, offs2, offs3, offs4, w1, wgs, rate, w4_words, w4_scales, out
+):
+    nc = tc.nc
+    with ExitStack() as ctx:
+        keep = ctx.enter_context(tc.tile_pool(name="keep", bufs=1))
+        work = ctx.enter_context(tc.tile_pool(name="work", bufs=2))
+        psum1 = ctx.enter_context(tc.psum_pool(name="psum1", bufs=4))
+        psum2 = ctx.enter_context(tc.psum_pool(name="psum2", bufs=3))
+
+        lists = {}
+
+        def load_list(name, src):
+            lists[name] = keep.tile([P, S // 16], U16, name=name)
+            nc.sync.dma_start(lists[name][:], src)
+
+        def entries(name, lo, hi):
+            return lists[name][:, lo // 16 : hi // 16]
+
+        tab_sc = keep.tile([P, T], U8, name="tab_sc", align_bytes=64)
+        nc.vector.memset(tab_sc[:].bitcast(I32), 0)
+        load_list("ions", offs)
+        for q in range(4):
+            nc.scalar.dma_start(
+                tab_sc[32 * q : 32 * q + 8, :].bitcast(I32), tab_scales[:, 4 * q : 4 * q + 4, :].bitcast(I32)
+            )
+        pages = [keep.tile([P, T2], F32, name="page0")]
+        nc.vector.memset(pages[0][:], 0.0)
+
+        tab_w = [
+            work.tile([P, T], U32, name="tab_w0", tag="wide", bufs=4, align_bytes=64),
+            work.tile([P, T], U32, name="tab_w1", tag="page1", bufs=1, align_bytes=64),
+        ]
+
+        def load_tab(a):
+            nc.sync.dma_start(tab_w[a][:].bitcast(I32), tab_words[a].rearrange("p t i -> p (t i)").bitcast(I32))
+
+        def load_rows(src, g, c):
+            raw = work.tile([P, PACK, HALF], F32, name="raw", tag="raw", bufs=3)
+            rows = src[KP * g : KP * (g + 1), HALF * c : HALF * (c + 1)]
+            nc.sync.dma_start(raw[:], rows.rearrange("(p j) c -> p j c", j=PACK))
+            return raw
+
+        site_w = [keep.tile([P, S], F32, name=f"site_w{t}") for t in range(PACK)]
+
+        def load_site_w(t):
+            rows = wgs.rearrange("(q t) j -> t q j", t=PACK)[t]
+            for q in range(4):
+                nc.sync.dma_start(site_w[t][32 * q : 32 * (q + 1), :], rows)
+
+        w1_raw = {}
+        load_tab(0)
+        w1_raw[0, 0] = load_rows(w1, 0, 0)
+        w1_raw[0, 1] = load_rows(w1, 1, 0)
+        load_tab(1)
+        load_list("sites", offs2)
+        load_site_w(0)
+        load_list("origins", offs3)
+        load_list("targets", offs4)
+        w1_raw[1, 0] = load_rows(w1, 0, 1)
+        w1_raw[1, 1] = load_rows(w1, 1, 1)
+        for t in range(1, PACK):
+            load_site_w(t)
+
+        w4_w = keep.tile([P, PASSES, 2 * N], U8, name="w4_w", align_bytes=64)
+        w4_sc = keep.tile([P, PASSES, N], U8, name="w4_sc", align_bytes=64)
+        nc.vector.memset(w4_sc[:].rearrange("p a n -> p (a n)").bitcast(I32), 0)
+        nc.sync.dma_start(w4_w[:].bitcast(I32), w4_words.rearrange("a p n -> p a n").bitcast(I32))
+        for q in range(4):
+            nc.sync.dma_start(
+                w4_sc[32 * q : 32 * q + 4, :, :].bitcast(I32),
+                w4_scales[:, 4 * q : 4 * q + 4, :].rearrange("a r n -> r a n").bitcast(I32),
+            )
+
+        got_sc = keep.tile([P, S], U8, name="got_sc", align_bytes=64)
+        nc.vector.tensor_copy(got_sc[:], tab_sc[:].indirect(entries("ions", 0, S)))
+        got_w0 = keep.tile([P, S], U32, name="got_w0", align_bytes=64)
+        nc.vector.tensor_copy(got_w0[:], tab_w[0][:].indirect(entries("ions", 0, S)))
+
+        w1_codes, w1_sc = {}, {}
+
+        def quantise_w1(b, a, on_vector, tag, bufs):
+            grouped = work.tile([P, PACK * HALF], BF16, name="grouped", tag=tag, bufs=bufs, align_bytes=64)
+            dst = grouped[:].rearrange("p (t m j) -> p m t j", t=PACK, j=PACK)
+            src = w1_raw[b, a][:].rearrange("p j (m t) -> p m t j", t=PACK)
+            if on_vector:
+                nc.vector.tensor_copy(dst, src)
+            else:
+                nc.scalar.copy(dst, src)
+            w1_codes[b, a] = keep.tile([P, HALF], U32, name=f"w1_codes{b}{a}", align_bytes=64)
+            w1_sc[b, a] = keep.tile([P, HALF], U8, name=f"w1_sc{b}{a}", align_bytes=64)
+            nc.vector.quantize_mx(out=w1_codes[b, a][:].bitcast(FP8X4), scales=w1_sc[b, a][:], in_=grouped[:])
+
+        quantise_w1(0, 0, False, "grouped", 1)
+        quantise_w1(0, 1, True, "page2", 1)
+
+        got_w1 = [keep.tile([P, HALF], U32, name=f"got_w1{i}", align_bytes=64) for i in range(2)]
+        for i in range(2):
+            nc.vector.tensor_copy(got_w1[i][:], tab_w[1][:].indirect(entries("ions", HALF * i, HALF * (i + 1))))
+
+        for tag in ("page1", "page2"):
+            pages.append(work.tile([P, T2], F32, name=tag, tag=tag, bufs=1, align_bytes=64))
+            nc.gpsimd.memset(pages[-1][:], 0.0)
+
+        feats = {}
+
+        def features(b, t):
+            feats[b, t] = keep.tile([P, S], F32, name=f"feats{b}{t}")
+            rows = slice(P * t, P * (t + 1))
+            for i in range(2):
+                cols = slice(HALF * i, HALF * (i + 1))
+                acc = psum1.tile([P, HALF], F32, name="acc1")
+                for a in range(PASSES):
+                    moving = got_w0[:, cols] if a == 0 else got_w1[i][:]
+                    nc.tensor.matmul_mx(
+                        out=acc[:],
+                        lhsT=w1_codes[b, a][:, rows].bitcast(FP8X4),
+                        lhsT_scale=w1_sc[b, a][:, rows],
+                        rhs=moving.bitcast(FP8X4),
+                        rhs_scale=got_sc[4 * a : P, cols],
+                        start=(a == 0),
+                        stop=(a == PASSES - 1),
+                    )
+                nc.scalar.activation(feats[b, t][:, cols], acc[:], ACT.Silu)
+
+        for t in range(PACK):
+            features(0, t)
+        quantise_w1(1, 0, False, "origin", 2)
+        quantise_w1(1, 1, False, "origin", 2)
+        for t in range(PACK):
+            features(1, t)
+
+        rate_il = {}
+        for b in range(PASSES):
+            for i in range(2):
+                raw = load_rows(rate, b, i)
+                woven = work.tile([P, HALF, PACK], F32, name="rate_il", tag="wide", bufs=4, align_bytes=64)
+                nc.scalar.copy(woven[:], raw[:].rearrange("p t m -> p m t"))
+                rate_il[b, i] = woven
+
+        def place(b, t, pieces):
+            page = pages[(PACK * b + t) % len(pages)]
+            width = S // pieces
+            for i in range(pieces):
+                lo, hi = width * i, width * (i + 1)
+                nc.vector.tensor_tensor(
+                    page[:].indirect(entries("sites", lo, hi)), feats[b, t][:, lo:hi], site_w[t][:, lo:hi], ALU.mult
+                )
+            return page
+
+        def fetch_origin(page, lo, hi):
+            origin = work.tile([P, hi - lo], F32, name="origin", tag="origin", bufs=2, align_bytes=64)
+            nc.vector.tensor_copy(origin[:], page[:].indirect(entries("origins", lo, hi)))
+            return origin
+
+        def differ(page, origin_cols, denom, t, lo, hi):
+            diff = work.tile([P, hi - lo], F32, name="diff", tag="diff", bufs=3)
+            nc.vector.tensor_tensor(diff[:], page[:].indirect(entries("targets", lo, hi)), origin_cols, ALU.subtract)
+            nc.scalar.activation(diff[:], diff[:], ACT.Square)
+            nc.scalar.activation(denom[:, t, lo:hi], diff[:], ACT.Square, bias=1.0)
+
+        z_mx = {}
+
+        def damp(b, denom, lo, hi):
+            width = hi - lo
+            damping = work.tile([P, width, PACK], F32, name="damping", tag="damping", bufs=4)
+            nc.scalar.activation(damping[:], denom[:, :, lo:hi].rearrange("p t m -> p m t"), ACT.Abs_reciprocal_sqrt)
+            z = work.tile([P, width * PACK], BF16, name="z", tag="z", bufs=2, align_bytes=64)
+            m0 = lo % HALF
+            nc.vector.tensor_tensor(
+                z[:],
+                damping[:].rearrange("p m t -> p (m t)"),
+                rate_il[b, lo // HALF][:, m0 : m0 + width, :].rearrange("p m t -> p (m t)"),
+                ALU.mult,
+            )
+            codes = keep.tile([P, width], U32, name=f"z_codes{b}_{lo}", align_bytes=64)
+            scales = keep.tile([P, width], U8, name=f"z_sc{b}_{lo}", align_bytes=64)
+            nc.vector.quantize_mx(out=codes[:].bitcast(FP8X4), scales=scales[:], in_=z[:])
+            for m in range(lo, hi, SUB):
+                z_mx[b, m] = (codes[:, m - lo : m - lo + SUB], scales[:, m - lo : m - lo + SUB])
+
+        def score(m0, on_vector):
+            acc = psum2.tile([P, NT, SUB], F32, name="acc2")
+            for n in range(NT):
+                for a in range(PASSES):
+                    codes, scales = z_mx[a, m0]
+                    nc.tensor.matmul_mx(
+                        out=acc[:, n, :],
+                        lhsT=w4_w[:, a, 2 * P * n : 2 * P * (n + 1)].bitcast(FP4X4),
+                        lhsT_scale=w4_sc[:, a, P * n : P * (n + 1)],
+                        rhs=codes.bitcast(FP8X4),
+                        rhs_scale=scales,
+                        start=(a == 0),
+                        stop=(a == PASSES - 1),
+                    )
+            staged = work.tile([P, NT, SUB], F32, name="staged", tag="staged", bufs=4)
+            if on_vector:
+                nc.vector.tensor_copy(staged[:], acc[:])
+            else:
+                nc.scalar.copy(staged[:], acc[:])
+            nc.sync.dma_start(out.rearrange("(n p) m -> p n m", p=P)[:, :, m0 : m0 + SUB], staged[:])
+
+        for b in range(PASSES):
+            denom = work.tile([P, PACK, HOPS], F32, name="denom", tag="denom", bufs=1)
+            last = b == PASSES - 1
+            for t in range(PACK - 2 if last else PACK):
+                page = place(b, t, 2 if (b, t) == (0, 0) else 1)
+                differ(page, fetch_origin(page, 0, HOPS)[:], denom, t, 0, HOPS)
+            if not last:
+                for lo in range(0, HOPS, CHUNK):
+                    damp(b, denom, lo, lo + CHUNK)
+            else:
+                tail = [(t, place(b, t, 1)) for t in (PACK - 2, PACK - 1)]
+                for lo in range(0, HOPS, CHUNK):
+                    origins = [fetch_origin(page, lo, lo + CHUNK) for t, page in tail]
+                    step = SUB if lo + CHUNK == HOPS else CHUNK
+                    for m in range(lo, lo + CHUNK, step):
+                        for (t, page), origin in zip(tail, origins):
+                            differ(page, origin[:, m - lo : m - lo + step], denom, t, m, m + step)
+                        damp(b, denom, m, m + step)
+        for m0 in range(0, HOPS, SUB):
+            score(m0, m0 + SUB == HOPS)

@@ -1,6 +1,7 @@
 from contextlib import ExitStack
 
 import concourse.mybir as mybir
+from concourse.masks import make_identity
 
 K, H, N, T, S, T2, HOPS = 1024, 1024, 384, 2048, 1024, 2048, 1024
 FLOPS = 2 * K * H * S + 2 * H * N * HOPS
@@ -22,8 +23,9 @@ KP = P * PACK
 PASSES = 2
 HALF = 512
 CHUNK = 256
-SUB = 128
 NT = N // P
+QUAD = P // PACK
+BLOCKS = H // P
 
 
 def tile_list_vacancy_hop_barriers_kernel(
@@ -33,8 +35,7 @@ def tile_list_vacancy_hop_barriers_kernel(
     with ExitStack() as ctx:
         keep = ctx.enter_context(tc.tile_pool(name="keep", bufs=1))
         work = ctx.enter_context(tc.tile_pool(name="work", bufs=2))
-        psum1 = ctx.enter_context(tc.psum_pool(name="psum1", bufs=4))
-        psum2 = ctx.enter_context(tc.psum_pool(name="psum2", bufs=3))
+        psum = ctx.enter_context(tc.psum_pool(name="psum", bufs=2))
 
         lists = {}
 
@@ -49,11 +50,13 @@ def tile_list_vacancy_hop_barriers_kernel(
         nc.vector.memset(tab_sc[:].bitcast(I32), 0)
         load_list("ions", offs)
         for q in range(4):
-            nc.scalar.dma_start(
+            nc.sync.dma_start(
                 tab_sc[32 * q : 32 * q + 8, :].bitcast(I32), tab_scales[:, 4 * q : 4 * q + 4, :].bitcast(I32)
             )
         pages = [keep.tile([P, T2], F32, name="page0")]
         nc.vector.memset(pages[0][:], 0.0)
+        ident = keep.tile([P, P], F32, name="ident")
+        make_identity(nc, ident[:])
 
         tab_w = [
             work.tile([P, T], U32, name="tab_w0", tag="wide", bufs=4, align_bytes=64),
@@ -63,32 +66,27 @@ def tile_list_vacancy_hop_barriers_kernel(
         def load_tab(a):
             nc.sync.dma_start(tab_w[a][:].bitcast(I32), tab_words[a].rearrange("p t i -> p (t i)").bitcast(I32))
 
-        def load_rows(src, g, c):
-            raw = work.tile([P, PACK, HALF], F32, name="raw", tag="raw", bufs=3)
-            rows = src[KP * g : KP * (g + 1), HALF * c : HALF * (c + 1)]
-            nc.sync.dma_start(raw[:], rows.rearrange("(p j) c -> p j c", j=PACK))
+        def load_rows(src, g, lo, hi, tag, bufs):
+            raw = work.tile([P, PACK, hi - lo], F32, name="raw", tag=tag, bufs=bufs)
+            nc.sync.dma_start(raw[:], src[KP * g : KP * (g + 1), lo:hi].rearrange("(p j) c -> p j c", j=PACK))
             return raw
 
-        site_w = [keep.tile([P, S], F32, name=f"site_w{t}") for t in range(PACK)]
-
-        def load_site_w(t):
-            rows = wgs.rearrange("(q t) j -> t q j", t=PACK)[t]
-            for q in range(4):
-                nc.sync.dma_start(site_w[t][32 * q : 32 * (q + 1), :], rows)
-
+        w1_cuts = [(0, P), (P, HALF), (HALF, H)]
         w1_raw = {}
         load_tab(0)
-        w1_raw[0, 0] = load_rows(w1, 0, 0)
-        w1_raw[0, 1] = load_rows(w1, 1, 0)
+        for a in range(PASSES):
+            w1_raw[0, a] = load_rows(w1, a, 0, P, "raw_head", 2)
         load_tab(1)
         load_list("sites", offs2)
-        load_site_w(0)
+        site_w = keep.tile([P, S], F32, name="site_w")
+        for lo in range(0, S, HALF):
+            nc.sync.dma_start(site_w[:, lo : lo + HALF], wgs[:, lo : lo + HALF])
+        for a in range(PASSES):
+            w1_raw[1, a] = load_rows(w1, a, P, HALF, "raw", 3)
         load_list("origins", offs3)
         load_list("targets", offs4)
-        w1_raw[1, 0] = load_rows(w1, 0, 1)
-        w1_raw[1, 1] = load_rows(w1, 1, 1)
-        for t in range(1, PACK):
-            load_site_w(t)
+        for a in range(PASSES):
+            w1_raw[2, a] = load_rows(w1, a, HALF, H, "raw", 3)
 
         w4_w = keep.tile([P, PASSES, 2 * N], U8, name="w4_w", align_bytes=64)
         w4_sc = keep.tile([P, PASSES, N], U8, name="w4_sc", align_bytes=64)
@@ -105,110 +103,126 @@ def tile_list_vacancy_hop_barriers_kernel(
         got_w0 = keep.tile([P, S], U32, name="got_w0", align_bytes=64)
         nc.vector.tensor_copy(got_w0[:], tab_w[0][:].indirect(entries("ions", 0, S)))
 
-        w1_codes, w1_sc = {}, {}
+        w1_mx = {}
 
-        def quantise_w1(b, a, on_vector, tag, bufs):
-            grouped = work.tile([P, PACK * HALF], BF16, name="grouped", tag=tag, bufs=bufs, align_bytes=64)
-            dst = grouped[:].rearrange("p (t m j) -> p m t j", t=PACK, j=PACK)
-            src = w1_raw[b, a][:].rearrange("p j (m t) -> p m t j", t=PACK)
-            if on_vector:
-                nc.vector.tensor_copy(dst, src)
-            else:
-                nc.scalar.copy(dst, src)
-            w1_codes[b, a] = keep.tile([P, HALF], U32, name=f"w1_codes{b}{a}", align_bytes=64)
-            w1_sc[b, a] = keep.tile([P, HALF], U8, name=f"w1_sc{b}{a}", align_bytes=64)
-            nc.vector.quantize_mx(out=w1_codes[b, a][:].bitcast(FP8X4), scales=w1_sc[b, a][:], in_=grouped[:])
+        def quantise_w1(cut, a, tag, bufs):
+            lo, hi = w1_cuts[cut]
+            grouped = work.tile([P, hi - lo, PACK], BF16, name="grouped", tag=tag, bufs=bufs, align_bytes=64)
+            nc.scalar.copy(
+                grouped[:].rearrange("p (c i) j -> p c j i", i=PACK),
+                w1_raw[cut, a][:].rearrange("p j (c i) -> p c j i", i=PACK),
+            )
+            codes = keep.tile([P, hi - lo], U32, name=f"w1_codes{cut}{a}", align_bytes=64)
+            scales = keep.tile([P, hi - lo], U8, name=f"w1_sc{cut}{a}", align_bytes=64)
+            c0 = 0
+            for width in {P: [P], HALF - P: [P, CHUNK], HALF: [HALF]}[hi - lo]:
+                nc.vector.quantize_mx(
+                    out=codes[:, c0 : c0 + width].bitcast(FP8X4),
+                    scales=scales[:, c0 : c0 + width],
+                    in_=grouped[:, c0 : c0 + width, :].rearrange("p c j -> p (c j)"),
+                )
+                c0 = c0 + width
+            for r in range(lo, hi, P):
+                w1_mx[r // P, a] = (codes[:, r - lo : r - lo + P], scales[:, r - lo : r - lo + P])
 
-        quantise_w1(0, 0, False, "grouped", 1)
-        quantise_w1(0, 1, True, "page2", 1)
+        for a in range(PASSES):
+            quantise_w1(0, a, "grouped_head", 2)
 
         got_w1 = [keep.tile([P, HALF], U32, name=f"got_w1{i}", align_bytes=64) for i in range(2)]
         for i in range(2):
             nc.vector.tensor_copy(got_w1[i][:], tab_w[1][:].indirect(entries("ions", HALF * i, HALF * (i + 1))))
 
-        for tag in ("page1", "page2"):
-            pages.append(work.tile([P, T2], F32, name=tag, tag=tag, bufs=1, align_bytes=64))
-            nc.gpsimd.memset(pages[-1][:], 0.0)
+        pages.append(work.tile([P, T2], F32, name="page1", tag="page1", bufs=1, align_bytes=64))
+        nc.gpsimd.memset(pages[1][:], 0.0)
 
         feats = {}
 
-        def features(b, t):
-            feats[b, t] = keep.tile([P, S], F32, name=f"feats{b}{t}")
-            rows = slice(P * t, P * (t + 1))
+        def features(k):
+            feats[k] = keep.tile([P, S], F32, name=f"feats{k}")
             for i in range(2):
                 cols = slice(HALF * i, HALF * (i + 1))
-                acc = psum1.tile([P, HALF], F32, name="acc1")
+                acc = psum.tile([P, HALF], F32, name="acc1", tag="acc", bufs=3)
                 for a in range(PASSES):
                     moving = got_w0[:, cols] if a == 0 else got_w1[i][:]
+                    codes, scales = w1_mx[k, a]
                     nc.tensor.matmul_mx(
                         out=acc[:],
-                        lhsT=w1_codes[b, a][:, rows].bitcast(FP8X4),
-                        lhsT_scale=w1_sc[b, a][:, rows],
+                        lhsT=codes.bitcast(FP8X4),
+                        lhsT_scale=scales,
                         rhs=moving.bitcast(FP8X4),
                         rhs_scale=got_sc[4 * a : P, cols],
                         start=(a == 0),
                         stop=(a == PASSES - 1),
                     )
-                nc.scalar.activation(feats[b, t][:, cols], acc[:], ACT.Silu)
+                nc.scalar.activation(feats[k][:, cols], acc[:], ACT.Silu)
 
-        for t in range(PACK):
-            features(0, t)
-        quantise_w1(1, 0, False, "origin", 2)
-        quantise_w1(1, 1, False, "origin", 2)
-        for t in range(PACK):
-            features(1, t)
-
-        rate_il = {}
-        for b in range(PASSES):
-            for i in range(2):
-                raw = load_rows(rate, b, i)
-                woven = work.tile([P, HALF, PACK], F32, name="rate_il", tag="wide", bufs=4, align_bytes=64)
-                nc.scalar.copy(woven[:], raw[:].rearrange("p t m -> p m t"))
-                rate_il[b, i] = woven
-
-        def place(b, t, pieces):
-            page = pages[(PACK * b + t) % len(pages)]
-            width = S // pieces
-            for i in range(pieces):
-                lo, hi = width * i, width * (i + 1)
+        def place(k):
+            page = pages[k % 2]
+            width = HALF if k == 0 else S
+            for lo in range(0, S, width):
+                hi = lo + width
                 nc.vector.tensor_tensor(
-                    page[:].indirect(entries("sites", lo, hi)), feats[b, t][:, lo:hi], site_w[t][:, lo:hi], ALU.mult
+                    page[:].indirect(entries("sites", lo, hi)), feats[k][:, lo:hi], site_w[:, lo:hi], ALU.mult
                 )
             return page
 
-        def fetch_origin(page, lo, hi):
-            origin = work.tile([P, hi - lo], F32, name="origin", tag="origin", bufs=2, align_bytes=64)
-            nc.vector.tensor_copy(origin[:], page[:].indirect(entries("origins", lo, hi)))
-            return origin
+        def origin_tile():
+            return work.tile([P, HOPS], F32, name="origin", tag="origin", bufs=1, align_bytes=64)
 
-        def differ(page, origin_cols, denom, t, lo, hi):
-            diff = work.tile([P, hi - lo], F32, name="diff", tag="diff", bufs=3)
-            nc.vector.tensor_tensor(diff[:], page[:].indirect(entries("targets", lo, hi)), origin_cols, ALU.subtract)
-            nc.scalar.activation(diff[:], diff[:], ACT.Square)
-            nc.scalar.activation(denom[:, t, lo:hi], diff[:], ACT.Square, bias=1.0)
+        def fetch_origins(page, origin, lo, hi):
+            nc.vector.tensor_copy(origin[:, lo:hi], page[:].indirect(entries("origins", lo, hi)))
+
+        def fetch_targets(page, lo):
+            target = work.tile([P, HALF], F32, name="target", tag="target", bufs=2)
+            nc.vector.tensor_scalar(
+                target[:], page[:].indirect(entries("targets", lo, lo + HALF)), -1.0, 0.0, ALU.mult, ALU.add
+            )
+            return target
+
+        def differ(k, denom, origin_cols, target_cols, lo, hi):
+            blocks = (hi - lo) // P
+            diff = psum.tile([P, blocks, P], F32, name="diff", tag="diff", bufs=2)
+            for j in range(blocks):
+                cols = slice(P * j, P * (j + 1))
+                nc.tensor.matmul(diff[:, j, :], origin_cols[:, cols], ident[:], start=True, stop=False, is_transpose=True)
+                nc.tensor.matmul(diff[:, j, :], target_cols[:, cols], ident[:], start=False, stop=True, is_transpose=True)
+            q0 = QUAD * (k % PACK)
+            part = denom[:, lo // P : hi // P, :, q0 : q0 + QUAD]
+            nc.scalar.activation(part, diff[:].rearrange("m j (q t) -> m j t q", t=PACK), ACT.Square)
+            nc.scalar.activation(part, part, ACT.Square, bias=1.0)
 
         z_mx = {}
 
-        def damp(b, denom, lo, hi):
+        dampings = {}
+
+        def invert(b, denom, lo):
+            damping = work.tile([P, HALF, PACK], F32, name="damping", tag="damping", bufs=3)
+            for m in range(0, HALF, P):
+                back = psum.tile([P, PACK, P], F32, name="back", tag="back", bufs=3)
+                for t in range(PACK):
+                    nc.tensor.transpose(back[:, t, :], denom[:, (lo + m) // P, t, :], ident[:])
+                nc.scalar.activation(
+                    damping[:, m : m + P, :], back[:].rearrange("p t m -> p m t"), ACT.Abs_reciprocal_sqrt
+                )
+            dampings[b, lo // HALF] = damping
+
+        def quantise_z(b, z, lo, hi):
             width = hi - lo
-            damping = work.tile([P, width, PACK], F32, name="damping", tag="damping", bufs=4)
-            nc.scalar.activation(damping[:], denom[:, :, lo:hi].rearrange("p t m -> p m t"), ACT.Abs_reciprocal_sqrt)
-            z = work.tile([P, width * PACK], BF16, name="z", tag="z", bufs=2, align_bytes=64)
-            m0 = lo % HALF
+            cols = slice(lo % HALF, lo % HALF + width)
             nc.vector.tensor_tensor(
-                z[:],
-                damping[:].rearrange("p m t -> p (m t)"),
-                rate_il[b, lo // HALF][:, m0 : m0 + width, :].rearrange("p m t -> p (m t)"),
+                z,
+                dampings[b, lo // HALF][:, cols, :].rearrange("p m t -> p (m t)"),
+                rate_il[b, lo // HALF][:, cols, :].rearrange("p m t -> p (m t)"),
                 ALU.mult,
             )
             codes = keep.tile([P, width], U32, name=f"z_codes{b}_{lo}", align_bytes=64)
             scales = keep.tile([P, width], U8, name=f"z_sc{b}_{lo}", align_bytes=64)
-            nc.vector.quantize_mx(out=codes[:].bitcast(FP8X4), scales=scales[:], in_=z[:])
-            for m in range(lo, hi, SUB):
-                z_mx[b, m] = (codes[:, m - lo : m - lo + SUB], scales[:, m - lo : m - lo + SUB])
+            nc.vector.quantize_mx(out=codes[:].bitcast(FP8X4), scales=scales[:], in_=z)
+            for m in range(lo, hi, P):
+                z_mx[b, m] = (codes[:, m - lo : m - lo + P], scales[:, m - lo : m - lo + P])
 
         def score(m0, on_vector):
-            acc = psum2.tile([P, NT, SUB], F32, name="acc2")
+            acc = psum.tile([P, NT, P], F32, name="acc2", tag="acc", bufs=3)
             for n in range(NT):
                 for a in range(PASSES):
                     codes, scales = z_mx[a, m0]
@@ -221,30 +235,54 @@ def tile_list_vacancy_hop_barriers_kernel(
                         start=(a == 0),
                         stop=(a == PASSES - 1),
                     )
-            staged = work.tile([P, NT, SUB], F32, name="staged", tag="staged", bufs=4)
+            staged = work.tile([P, NT, P], F32, name="staged", tag="staged", bufs=8)
             if on_vector:
                 nc.vector.tensor_copy(staged[:], acc[:])
             else:
                 nc.scalar.copy(staged[:], acc[:])
-            nc.sync.dma_start(out.rearrange("(n p) m -> p n m", p=P)[:, :, m0 : m0 + SUB], staged[:])
+            nc.sync.dma_start(out.rearrange("(n p) m -> p n m", p=P)[:, :, m0 : m0 + P], staged[:])
 
+        def whole_block(k, denom):
+            page = place(k)
+            origin = origin_tile()
+            width = HALF if k == BLOCKS - 1 else HOPS
+            for lo in range(0, HOPS, HALF):
+                if lo % width == 0:
+                    fetch_origins(page, origin, lo, lo + width)
+                differ(k, denom, origin[:, lo : lo + HALF], fetch_targets(page, lo)[:], lo, lo + HALF)
+
+        features(0)
+        quantise_w1(1, 0, "grouped", 1)
+        quantise_w1(1, 1, "origin", 1)
+        for k in range(1, PACK):
+            features(k)
+
+        denoms = [work.tile([P, HOPS // P, PACK, P], F32, name="denom", tag="denom", bufs=2) for b in range(PASSES)]
+        whole_block(0, denoms[0])
+        quantise_w1(2, 0, "grouped", 1)
+        quantise_w1(2, 1, "origin", 1)
+        for k in range(PACK, BLOCKS):
+            features(k)
+
+        rate_il = {}
         for b in range(PASSES):
-            denom = work.tile([P, PACK, HOPS], F32, name="denom", tag="denom", bufs=1)
-            last = b == PASSES - 1
-            for t in range(PACK - 2 if last else PACK):
-                page = place(b, t, 2 if (b, t) == (0, 0) else 1)
-                differ(page, fetch_origin(page, 0, HOPS)[:], denom, t, 0, HOPS)
-            if not last:
-                for lo in range(0, HOPS, CHUNK):
-                    damp(b, denom, lo, lo + CHUNK)
-            else:
-                tail = [(t, place(b, t, 1)) for t in (PACK - 2, PACK - 1)]
-                for lo in range(0, HOPS, CHUNK):
-                    origins = [fetch_origin(page, lo, lo + CHUNK) for t, page in tail]
-                    step = SUB if lo + CHUNK == HOPS else CHUNK
-                    for m in range(lo, lo + CHUNK, step):
-                        for (t, page), origin in zip(tail, origins):
-                            differ(page, origin[:, m - lo : m - lo + step], denom, t, m, m + step)
-                        damp(b, denom, m, m + step)
-        for m0 in range(0, HOPS, SUB):
-            score(m0, m0 + SUB == HOPS)
+            for i in range(2):
+                raw = load_rows(rate, b, HALF * i, HALF * (i + 1), "raw", 3)
+                woven = work.tile([P, HALF, PACK], F32, name="rate_il", tag="wide", bufs=4, align_bytes=64)
+                nc.scalar.copy(woven[:], raw[:].rearrange("p t m -> p m t"))
+                rate_il[b, i] = woven
+
+        for k in range(1, BLOCKS):
+            whole_block(k, denoms[k // PACK])
+            if k % PACK == PACK - 1:
+                for lo in range(0, HOPS, HALF):
+                    invert(k // PACK, denoms[k // PACK], lo)
+
+        z0 = work.tile([P, HOPS * PACK], BF16, name="z0", tag="page1", bufs=1, align_bytes=64)
+        for lo in range(0, HOPS, HALF):
+            quantise_z(0, z0[:, PACK * lo : PACK * (lo + HALF)], lo, lo + HALF)
+        for lo, hi in ((0, 256), (256, 512), (512, 768), (768, 896), (896, 1024)):
+            z1 = work.tile([P, (hi - lo) * PACK], BF16, name="z1", tag="z1", bufs=2, align_bytes=64)
+            quantise_z(1, z1[:], lo, hi)
+        for m0 in range(0, HOPS, P):
+            score(m0, m0 + P == HOPS)

@@ -53,7 +53,7 @@ def tile_list_vacancy_hop_barriers_kernel(
             nc.sync.dma_start(
                 tab_sc[32 * q : 32 * q + 8, :].bitcast(I32), tab_scales[:, 4 * q : 4 * q + 4, :].bitcast(I32)
             )
-        pages = [keep.tile([P, T2], F32, name="page0")]
+        pages = [work.tile([P, T2], F32, name="page0", tag="page0", bufs=1, align_bytes=64)]
         nc.vector.memset(pages[0][:], 0.0)
         ident = keep.tile([P, P], F32, name="ident")
         make_identity(nc, ident[:])
@@ -138,7 +138,7 @@ def tile_list_vacancy_hop_barriers_kernel(
         feats = {}
 
         def features(k):
-            feats[k] = keep.tile([P, S], F32, name=f"feats{k}")
+            feats[k] = keep.tile([P, S], F32, name=f"feats{k}", align_bytes=64)
             for i in range(2):
                 cols = slice(HALF * i, HALF * (i + 1))
                 acc = psum.tile([P, HALF], F32, name="acc1", tag="acc", bufs=3)
@@ -157,7 +157,7 @@ def tile_list_vacancy_hop_barriers_kernel(
                 nc.scalar.activation(feats[k][:, cols], acc[:], ACT.Silu)
 
         def place(k):
-            page = pages[k % 2]
+            page = pages[min(k, BLOCKS - 2) % 2]
             width = HALF if k == 0 else S
             for lo in range(0, S, width):
                 hi = lo + width
@@ -181,7 +181,7 @@ def tile_list_vacancy_hop_barriers_kernel(
 
         def differ(k, denom, origin_cols, target_cols, lo, hi):
             blocks = (hi - lo) // P
-            diff = psum.tile([P, blocks, P], F32, name="diff", tag="diff", bufs=2)
+            diff = psum.tile([P, blocks, P], F32, name="diff", tag="turn", bufs=5)
             for j in range(blocks):
                 cols = slice(P * j, P * (j + 1))
                 nc.tensor.matmul(diff[:, j, :], origin_cols[:, cols], ident[:], start=True, stop=False, is_transpose=True)
@@ -190,41 +190,44 @@ def tile_list_vacancy_hop_barriers_kernel(
             part = denom[:, lo // P : hi // P, :, q0 : q0 + QUAD]
             nc.scalar.activation(part, diff[:].rearrange("m j (q t) -> m j t q", t=PACK), ACT.Square)
             nc.scalar.activation(part, part, ACT.Square, bias=1.0)
+            if k >= PACK:
+                nc.scalar.activation(part, part, ACT.Abs_reciprocal_sqrt)
 
         z_mx = {}
 
         dampings = {}
 
-        def invert(b, denom, lo):
-            damping = work.tile([P, HALF, PACK], F32, name="damping", tag="damping", bufs=3)
-            for m in range(0, HALF, P):
-                back = psum.tile([P, PACK, P], F32, name="back", tag="back", bufs=3)
+        def invert(b, denom, lo, hi):
+            if lo % HALF == 0:
+                dampings[b, lo // HALF] = work.tile([P, HALF, PACK], F32, name="damping", tag="damping", bufs=2)
+            damping = dampings[b, lo // HALF]
+            for m in range(lo, hi, P):
+                back = psum.tile([P, PACK, P], F32, name="back", tag="turn", bufs=5)
                 for t in range(PACK):
-                    nc.tensor.transpose(back[:, t, :], denom[:, (lo + m) // P, t, :], ident[:])
+                    nc.tensor.transpose(back[:, t, :], denom[:, m // P, t, :], ident[:])
                 nc.scalar.activation(
-                    damping[:, m : m + P, :], back[:].rearrange("p t m -> p m t"), ACT.Abs_reciprocal_sqrt
+                    damping[:, m % HALF : m % HALF + P, :], back[:].rearrange("p t m -> p m t"), ACT.Abs_reciprocal_sqrt
                 )
-            dampings[b, lo // HALF] = damping
 
-        def quantise_z(b, z, lo, hi):
-            width = hi - lo
-            cols = slice(lo % HALF, lo % HALF + width)
-            nc.vector.tensor_tensor(
+        def weigh(engine, b, z, lo, hi):
+            cols = slice(lo % HALF, lo % HALF + hi - lo)
+            engine.tensor_tensor(
                 z,
                 dampings[b, lo // HALF][:, cols, :].rearrange("p m t -> p (m t)"),
                 rate_il[b, lo // HALF][:, cols, :].rearrange("p m t -> p (m t)"),
                 ALU.mult,
             )
-            codes = keep.tile([P, width], U32, name=f"z_codes{b}_{lo}", align_bytes=64)
-            scales = keep.tile([P, width], U8, name=f"z_sc{b}_{lo}", align_bytes=64)
-            nc.vector.quantize_mx(out=codes[:].bitcast(FP8X4), scales=scales[:], in_=z)
+
+        def quantise_z(b, z, codes, lo, hi):
+            scales = keep.tile([P, hi - lo], U8, name=f"z_sc{b}_{lo}", align_bytes=64)
+            nc.vector.quantize_mx(out=codes.bitcast(FP8X4), scales=scales[:], in_=z)
             for m in range(lo, hi, P):
                 z_mx[b, m] = (codes[:, m - lo : m - lo + P], scales[:, m - lo : m - lo + P])
 
         def score(m0, on_vector):
             acc = psum.tile([P, NT, P], F32, name="acc2", tag="acc", bufs=3)
             for n in range(NT):
-                for a in range(PASSES):
+                for a in reversed(range(PASSES)):
                     codes, scales = z_mx[a, m0]
                     nc.tensor.matmul_mx(
                         out=acc[:, n, :],
@@ -232,8 +235,8 @@ def tile_list_vacancy_hop_barriers_kernel(
                         lhsT_scale=w4_sc[:, a, P * n : P * (n + 1)],
                         rhs=codes.bitcast(FP8X4),
                         rhs_scale=scales,
-                        start=(a == 0),
-                        stop=(a == PASSES - 1),
+                        start=(a == PASSES - 1),
+                        stop=(a == 0),
                     )
             staged = work.tile([P, NT, P], F32, name="staged", tag="staged", bufs=8)
             if on_vector:
@@ -272,17 +275,46 @@ def tile_list_vacancy_hop_barriers_kernel(
                 nc.scalar.copy(woven[:], raw[:].rearrange("p t m -> p m t"))
                 rate_il[b, i] = woven
 
-        for k in range(1, BLOCKS):
-            whole_block(k, denoms[k // PACK])
-            if k % PACK == PACK - 1:
-                for lo in range(0, HOPS, HALF):
-                    invert(k // PACK, denoms[k // PACK], lo)
 
-        z0 = work.tile([P, HOPS * PACK], BF16, name="z0", tag="page1", bufs=1, align_bytes=64)
+        def block_and_inverse(k):
+            b = k // PACK
+            last = k == BLOCKS - 1
+            page = place(k)
+            origin = origin_tile()
+            width = CHUNK if last else HOPS
+            for lo in range(0, HOPS, HALF):
+                target = fetch_targets(page, lo)
+                for m in range(lo, lo + HALF, min(width, HALF)):
+                    if m % width == 0:
+                        fetch_origins(page, origin, m, m + width)
+                    hi = m + min(width, HALF)
+                    differ(k, denoms[b], origin[:, m:hi], target[:, m - lo : hi - lo], m, hi)
+                    if k == PACK - 1:
+                        invert(b, denoms[b], m, hi)
+
+        for k in range(1, BLOCKS):
+            if k == BLOCKS - 1:
+                z0 = keep.tile([P, HOPS * PACK], BF16, name="z0", tag=f"feats{k - 1}", align_bytes=64)
+                for lo in range(0, HOPS, HALF):
+                    weigh(nc.gpsimd, 0, z0[:, PACK * lo : PACK * (lo + HALF)], lo, lo + HALF)
+            block_and_inverse(k)
+
+        codes0 = work.tile([P, HOPS], U32, name="codes0", tag="page0", bufs=1, align_bytes=64)
         for lo in range(0, HOPS, HALF):
-            quantise_z(0, z0[:, PACK * lo : PACK * (lo + HALF)], lo, lo + HALF)
+            quantise_z(0, z0[:, PACK * lo : PACK * (lo + HALF)], codes0[:, lo : lo + HALF], lo, lo + HALF)
         for lo, hi in ((0, 256), (256, 512), (512, 768), (768, 896), (896, 1024)):
-            z1 = work.tile([P, (hi - lo) * PACK], BF16, name="z1", tag="z1", bufs=2, align_bytes=64)
-            quantise_z(1, z1[:], lo, hi)
+            z1 = work.tile([P, hi - lo, PACK], BF16, name="z1", tag="z1", bufs=2, align_bytes=64)
+            for m in range(lo, hi, P):
+                back = psum.tile([P, PACK, P], F32, name="back", tag="turn", bufs=5)
+                for t in range(PACK):
+                    nc.tensor.transpose(back[:, t, :], denoms[1][:, m // P, t, :], ident[:])
+                nc.vector.tensor_tensor(
+                    z1[:, m - lo : m - lo + P, :],
+                    back[:].rearrange("p t m -> p m t"),
+                    rate_il[1, m // HALF][:, m % HALF : m % HALF + P, :],
+                    ALU.mult,
+                )
+            codes1 = keep.tile([P, hi - lo], U32, name=f"codes1_{lo}", align_bytes=64)
+            quantise_z(1, z1[:].rearrange("p m t -> p (m t)"), codes1[:], lo, hi)
         for m0 in range(0, HOPS, P):
             score(m0, m0 + P == HOPS)

@@ -158,6 +158,11 @@ def tile_list_vacancy_hop_barriers_kernel(
 
         def place(k):
             page = pages[min(k, BLOCKS - 2) % 2]
+            if k >= PACK:
+                weighted = keep.tile([P, S], F32, name="weighted", tag=f"feats{PACK - 1}", align_bytes=64)
+                nc.gpsimd.tensor_tensor(weighted[:], feats[k][:], site_w[:], ALU.mult)
+                nc.vector.tensor_copy(page[:].indirect(entries("sites", 0, S)), weighted[:])
+                return page
             width = HALF if k == 0 else S
             for lo in range(0, S, width):
                 hi = lo + width
@@ -166,14 +171,14 @@ def tile_list_vacancy_hop_barriers_kernel(
                 )
             return page
 
-        def origin_tile():
-            return work.tile([P, HOPS], F32, name="origin", tag="origin", bufs=1, align_bytes=64)
+        def origin_tile(tag):
+            return work.tile([P, HOPS], F32, name="origin", tag=tag, bufs=1, align_bytes=64)
 
         def fetch_origins(page, origin, lo, hi):
             nc.vector.tensor_copy(origin[:, lo:hi], page[:].indirect(entries("origins", lo, hi)))
 
         def fetch_targets(page, lo):
-            target = work.tile([P, HALF], F32, name="target", tag="target", bufs=2)
+            target = work.tile([P, HALF], F32, name="target", tag="target", bufs=3)
             nc.vector.tensor_scalar(
                 target[:], page[:].indirect(entries("targets", lo, lo + HALF)), -1.0, 0.0, ALU.mult, ALU.add
             )
@@ -247,7 +252,7 @@ def tile_list_vacancy_hop_barriers_kernel(
 
         def whole_block(k, denom):
             page = place(k)
-            origin = origin_tile()
+            origin = origin_tile("origin")
             width = HALF if k == BLOCKS - 1 else HOPS
             for lo in range(0, HOPS, HALF):
                 if lo % width == 0:
@@ -280,7 +285,7 @@ def tile_list_vacancy_hop_barriers_kernel(
             b = k // PACK
             last = k == BLOCKS - 1
             page = place(k)
-            origin = origin_tile()
+            origin = origin_tile("last_origin" if last else "origin")
             width = CHUNK if last else HOPS
             for lo in range(0, HOPS, HALF):
                 target = fetch_targets(page, lo)
@@ -292,16 +297,17 @@ def tile_list_vacancy_hop_barriers_kernel(
                     if k == PACK - 1:
                         invert(b, denoms[b], m, hi)
 
+        z0 = []
         for k in range(1, BLOCKS):
-            if k == BLOCKS - 1:
-                z0 = keep.tile([P, HOPS * PACK], BF16, name="z0", tag=f"feats{k - 1}", align_bytes=64)
-                for lo in range(0, HOPS, HALF):
-                    weigh(nc.gpsimd, 0, z0[:, PACK * lo : PACK * (lo + HALF)], lo, lo + HALF)
             block_and_inverse(k)
+            if k >= BLOCKS - 2:
+                lo = HALF * len(z0)
+                z0.append(keep.tile([P, HALF * PACK], BF16, name="z0", tag=f"feats{k}", align_bytes=64))
+                weigh(nc.gpsimd, 0, z0[-1][:], lo, lo + HALF)
 
         codes0 = work.tile([P, HOPS], U32, name="codes0", tag="page0", bufs=1, align_bytes=64)
         for lo in range(0, HOPS, HALF):
-            quantise_z(0, z0[:, PACK * lo : PACK * (lo + HALF)], codes0[:, lo : lo + HALF], lo, lo + HALF)
+            quantise_z(0, z0[lo // HALF][:], codes0[:, lo : lo + HALF], lo, lo + HALF)
         for lo, hi in ((0, 256), (256, 512), (512, 768), (768, 896), (896, 1024)):
             z1 = work.tile([P, hi - lo, PACK], BF16, name="z1", tag="z1", bufs=2, align_bytes=64)
             for m in range(lo, hi, P):

@@ -49,10 +49,11 @@ def tile_list_vacancy_hop_barriers_kernel(
         tab_sc = keep.tile([P, T], U8, name="tab_sc", align_bytes=64)
         nc.vector.memset(tab_sc[:].bitcast(I32), 0)
         load_list("ions", offs)
+        landed_sc = keep.tile([P, T], U8, name="landed_sc", align_bytes=64)
         for q in range(4):
-            nc.sync.dma_start(
-                tab_sc[32 * q : 32 * q + 8, :].bitcast(I32), tab_scales[:, 4 * q : 4 * q + 4, :].bitcast(I32)
-            )
+            rows = slice(32 * q, 32 * q + 8)
+            nc.sync.dma_start(landed_sc[rows, :].bitcast(I32), tab_scales[:, 4 * q : 4 * q + 4, :].bitcast(I32))
+            nc.vector.tensor_copy(tab_sc[rows, :].bitcast(I32), landed_sc[rows, :].bitcast(I32))
         pages = [work.tile([P, T2], F32, name="page0", tag="page0", bufs=1, align_bytes=64)]
         nc.vector.memset(pages[0][:], 0.0)
         ident = keep.tile([P, P], F32, name="ident")

@@ -22,10 +22,12 @@ PACK = 4
 KP = P * PACK
 PASSES = 2
 HALF = 512
-CHUNK = 256
 NT = N // P
 QUAD = P // PACK
 BLOCKS = H // P
+LAST = BLOCKS - 1
+PAGES = 2
+TAIL_CUTS = ((0, 256), (256, 512), (512, 768), (768, 896), (896, 1024))
 
 
 def tile_list_vacancy_hop_barriers_kernel(
@@ -34,8 +36,10 @@ def tile_list_vacancy_hop_barriers_kernel(
     nc = tc.nc
     with ExitStack() as ctx:
         keep = ctx.enter_context(tc.tile_pool(name="keep", bufs=1))
-        work = ctx.enter_context(tc.tile_pool(name="work", bufs=2))
         psum = ctx.enter_context(tc.psum_pool(name="psum", bufs=2))
+
+        def sb(shape, dtype, name, tag=None, bufs=1):
+            return keep.tile(shape, dtype, name=name, tag=tag or name, bufs=bufs, align_bytes=64)
 
         lists = {}
 
@@ -46,103 +50,114 @@ def tile_list_vacancy_hop_barriers_kernel(
         def entries(name, lo, hi):
             return lists[name][:, lo // 16 : hi // 16]
 
-        tab_sc = keep.tile([P, T], U8, name="tab_sc", align_bytes=64)
+        tab_sc = sb([P, T], U8, "tab_sc")
         nc.vector.memset(tab_sc[:].bitcast(I32), 0)
         load_list("ions", offs)
-        landed_sc = keep.tile([P, T], U8, name="landed_sc", align_bytes=64)
+        landed_sc = sb([P, T], U8, "landed_sc")
         for q in range(4):
             rows = slice(32 * q, 32 * q + 8)
             nc.sync.dma_start(landed_sc[rows, :].bitcast(I32), tab_scales[:, 4 * q : 4 * q + 4, :].bitcast(I32))
             nc.vector.tensor_copy(tab_sc[rows, :].bitcast(I32), landed_sc[rows, :].bitcast(I32))
-        pages = [work.tile([P, T2], F32, name="page0", tag="page0", bufs=1, align_bytes=64)]
+        pages = [sb([P, T2], F32, "page0")]
         nc.vector.memset(pages[0][:], 0.0)
-        ident = keep.tile([P, P], F32, name="ident")
+        ident = sb([P, P], F32, "ident")
         make_identity(nc, ident[:])
 
-        tab_w = [
-            work.tile([P, T], U32, name="tab_w0", tag="wide", bufs=4, align_bytes=64),
-            work.tile([P, T], U32, name="tab_w1", tag="page1", bufs=1, align_bytes=64),
-        ]
+        tab_w = [sb([P, T], U32, "tab_w0", tag="page1"), sb([P, T], U32, "tab_w1", tag="z0_turned")]
 
         def load_tab(a):
             nc.sync.dma_start(tab_w[a][:].bitcast(I32), tab_words[a].rearrange("p t i -> p (t i)").bitcast(I32))
 
-        def load_rows(src, g, lo, hi, tag, bufs):
-            raw = work.tile([P, PACK, hi - lo], F32, name="raw", tag=tag, bufs=bufs)
-            nc.sync.dma_start(raw[:], src[KP * g : KP * (g + 1), lo:hi].rearrange("(p j) c -> p j c", j=PACK))
+        def load_w1(a, lo, hi):
+            raw = sb([P, PACK, hi - lo], F32, f"raw{lo}_{a}")
+            nc.sync.dma_start(raw[:], w1[KP * a : KP * (a + 1), lo:hi].rearrange("(p j) c -> p j c", j=PACK))
             return raw
 
-        w1_cuts = [(0, P), (P, HALF), (HALF, H)]
-        w1_raw = {}
         load_tab(0)
-        for a in range(PASSES):
-            w1_raw[0, a] = load_rows(w1, a, 0, P, "raw_head", 2)
+        raw_head = [load_w1(a, 0, P) for a in range(PASSES)]
         load_tab(1)
         load_list("sites", offs2)
-        site_w = keep.tile([P, S], F32, name="site_w")
+        site_w = sb([P, S], F32, "site_w")
         for lo in range(0, S, HALF):
             nc.sync.dma_start(site_w[:, lo : lo + HALF], wgs[:, lo : lo + HALF])
-        for a in range(PASSES):
-            w1_raw[1, a] = load_rows(w1, a, P, HALF, "raw", 3)
+        raw_mid = [load_w1(a, P, HALF) for a in range(PASSES)]
         load_list("origins", offs3)
         load_list("targets", offs4)
-        for a in range(PASSES):
-            w1_raw[2, a] = load_rows(w1, a, HALF, H, "raw", 3)
+        raw_end = [load_w1(a, HALF, H) for a in range(PASSES)]
+        rate0 = [sb([P, HOPS], F32, f"rate0_{k}") for k in range(PACK)]
+        for k in range(PACK):
+            nc.sync.dma_start(rate0[k][:], rate[P * k : P * (k + 1), :])
+        dealt_w = sb([P, PACK, S], F32, "dealt_w")
+        for q in range(PACK):
+            nc.sync.dma_start(dealt_w[QUAD * q : QUAD * (q + 1), :, :], wgs.rearrange("(q t) j -> q t j", t=PACK))
+        rate1 = [sb([P, HOPS], F32, f"rate1_{t}") for t in range(PACK)]
+        for t in range(PACK):
+            nc.sync.dma_start(rate1[t][:], rate[KP:H, :].rearrange("(p t) m -> p t m", t=PACK)[:, t, :])
 
-        w4_w = keep.tile([P, PASSES, 2 * N], U8, name="w4_w", align_bytes=64)
-        w4_sc = keep.tile([P, PASSES, N], U8, name="w4_sc", align_bytes=64)
-        nc.vector.memset(w4_sc[:].rearrange("p a n -> p (a n)").bitcast(I32), 0)
+        w4_w = sb([P, PASSES, 2 * N], U8, "w4_w")
         nc.sync.dma_start(w4_w[:].bitcast(I32), w4_words.rearrange("a p n -> p a n").bitcast(I32))
+        w4_sc = sb([P, PASSES, N], U8, "w4_sc")
+        nc.vector.memset(w4_sc[:].rearrange("p a n -> p (a n)").bitcast(I32), 0)
         for q in range(4):
             nc.sync.dma_start(
                 w4_sc[32 * q : 32 * q + 4, :, :].bitcast(I32),
                 w4_scales[:, 4 * q : 4 * q + 4, :].rearrange("a r n -> r a n").bitcast(I32),
             )
 
-        got_sc = keep.tile([P, S], U8, name="got_sc", align_bytes=64)
+        got_sc = sb([P, S], U8, "got_sc")
         nc.vector.tensor_copy(got_sc[:], tab_sc[:].indirect(entries("ions", 0, S)))
-        got_w0 = keep.tile([P, S], U32, name="got_w0", align_bytes=64)
+        got_w0 = sb([P, S], U32, "got_w0")
         nc.vector.tensor_copy(got_w0[:], tab_w[0][:].indirect(entries("ions", 0, S)))
 
         w1_mx = {}
 
-        def quantise_w1(cut, a, tag, bufs):
-            lo, hi = w1_cuts[cut]
-            grouped = work.tile([P, hi - lo, PACK], BF16, name="grouped", tag=tag, bufs=bufs, align_bytes=64)
-            nc.scalar.copy(
-                grouped[:].rearrange("p (c i) j -> p c j i", i=PACK),
-                w1_raw[cut, a][:].rearrange("p j (c i) -> p c j i", i=PACK),
+        def quantise_w1(name, raws, first, blocks, c0, dealt):
+            width = P * blocks
+            grouped = sb([P, PASSES, width, PACK], BF16, name)
+            for a in range(PASSES):
+                src = raws[a][:, :, c0 : c0 + width]
+                if dealt:
+                    nc.scalar.copy(
+                        grouped[:, a].rearrange("p (t m) j -> p m t j", t=PACK),
+                        src.rearrange("p j (m t) -> p m t j", t=PACK),
+                    )
+                else:
+                    nc.scalar.copy(
+                        grouped[:, a].rearrange("p (c i) j -> p c j i", i=PACK),
+                        src.rearrange("p j (c i) -> p c j i", i=PACK),
+                    )
+            codes = sb([P, PASSES * width], U32, name + "_codes")
+            scales = sb([P, PASSES * width], U8, name + "_sc")
+            nc.vector.quantize_mx(
+                out=codes[:].bitcast(FP8X4), scales=scales[:], in_=grouped[:].rearrange("p a c j -> p (a c j)")
             )
-            codes = keep.tile([P, hi - lo], U32, name=f"w1_codes{cut}{a}", align_bytes=64)
-            scales = keep.tile([P, hi - lo], U8, name=f"w1_sc{cut}{a}", align_bytes=64)
-            c0 = 0
-            for width in {P: [P], HALF - P: [P, CHUNK], HALF: [HALF]}[hi - lo]:
-                nc.vector.quantize_mx(
-                    out=codes[:, c0 : c0 + width].bitcast(FP8X4),
-                    scales=scales[:, c0 : c0 + width],
-                    in_=grouped[:, c0 : c0 + width, :].rearrange("p c j -> p (c j)"),
-                )
-                c0 = c0 + width
-            for r in range(lo, hi, P):
-                w1_mx[r // P, a] = (codes[:, r - lo : r - lo + P], scales[:, r - lo : r - lo + P])
+            for a in range(PASSES):
+                for b in range(blocks):
+                    cols = slice(width * a + P * b, width * a + P * (b + 1))
+                    w1_mx[first + b, a] = (codes[:, cols], scales[:, cols])
 
-        for a in range(PASSES):
-            quantise_w1(0, a, "grouped_head", 2)
+        quantise_w1("g0", raw_head, 0, 1, 0, False)
 
-        got_w1 = [keep.tile([P, HALF], U32, name=f"got_w1{i}", align_bytes=64) for i in range(2)]
+        got_w1 = [sb([P, HALF], U32, f"got_w1{i}") for i in range(2)]
         for i in range(2):
             nc.vector.tensor_copy(got_w1[i][:], tab_w[1][:].indirect(entries("ions", HALF * i, HALF * (i + 1))))
 
-        pages.append(work.tile([P, T2], F32, name="page1", tag="page1", bufs=1, align_bytes=64))
+        pages.append(sb([P, T2], F32, "page1"))
         nc.gpsimd.memset(pages[1][:], 0.0)
 
         feats = {}
 
+        def feats_tag(k):
+            return f"raw512_{k - 1}" if k in (1, 2) else f"feats{k}"
+
+        def ring(shape, name):
+            return psum.tile(shape, F32, name=name, tag="ring", bufs=2)
+
         def features(k):
-            feats[k] = keep.tile([P, S], F32, name=f"feats{k}", align_bytes=64)
+            feats[k] = sb([P, S], F32, f"feats{k}", tag=feats_tag(k))
             for i in range(2):
                 cols = slice(HALF * i, HALF * (i + 1))
-                acc = psum.tile([P, HALF], F32, name="acc1", tag="acc", bufs=3)
+                acc = ring([P, HALF], "acc1")
                 for a in range(PASSES):
                     moving = got_w0[:, cols] if a == 0 else got_w1[i][:]
                     codes, scales = w1_mx[k, a]
@@ -157,171 +172,224 @@ def tile_list_vacancy_hop_barriers_kernel(
                     )
                 nc.scalar.activation(feats[k][:, cols], acc[:], ACT.Silu)
 
+        def weights(k):
+            return site_w[:] if k < PACK else dealt_w[:, k - PACK, :]
+
+        weighted = {}
+
+        def preweigh(k, tag):
+            weighted[k] = sb([P, S], F32, "weighted", tag=tag)
+            nc.gpsimd.tensor_tensor(weighted[k][:], feats[k][:], weights(k), ALU.mult)
+
         def place(k):
-            page = pages[min(k, BLOCKS - 2) % 2]
-            if k >= PACK:
-                weighted = keep.tile([P, S], F32, name="weighted", tag=f"feats{PACK - 1}", align_bytes=64)
-                nc.gpsimd.tensor_tensor(weighted[:], feats[k][:], site_w[:], ALU.mult)
-                nc.vector.tensor_copy(page[:].indirect(entries("sites", 0, S)), weighted[:])
-                return page
+            page = pages[k % PAGES]
+            if k in weighted:
+                nc.vector.tensor_copy(page[:].indirect(entries("sites", 0, S)), weighted[k][:])
+                return
             width = HALF if k == 0 else S
             for lo in range(0, S, width):
                 hi = lo + width
                 nc.vector.tensor_tensor(
-                    page[:].indirect(entries("sites", lo, hi)), feats[k][:, lo:hi], site_w[:, lo:hi], ALU.mult
-                )
-            return page
-
-        def origin_tile(tag):
-            return work.tile([P, HOPS], F32, name="origin", tag=tag, bufs=1, align_bytes=64)
-
-        def fetch_origins(page, origin, lo, hi):
-            nc.vector.tensor_copy(origin[:, lo:hi], page[:].indirect(entries("origins", lo, hi)))
-
-        def fetch_targets(page, lo):
-            target = work.tile([P, HALF], F32, name="target", tag="target", bufs=3)
-            nc.vector.tensor_scalar(
-                target[:], page[:].indirect(entries("targets", lo, lo + HALF)), -1.0, 0.0, ALU.mult, ALU.add
-            )
-            return target
-
-        def differ(k, denom, origin_cols, target_cols, lo, hi):
-            blocks = (hi - lo) // P
-            diff = psum.tile([P, blocks, P], F32, name="diff", tag="turn", bufs=5)
-            for j in range(blocks):
-                cols = slice(P * j, P * (j + 1))
-                nc.tensor.matmul(diff[:, j, :], origin_cols[:, cols], ident[:], start=True, stop=False, is_transpose=True)
-                nc.tensor.matmul(diff[:, j, :], target_cols[:, cols], ident[:], start=False, stop=True, is_transpose=True)
-            q0 = QUAD * (k % PACK)
-            part = denom[:, lo // P : hi // P, :, q0 : q0 + QUAD]
-            nc.scalar.activation(part, diff[:].rearrange("m j (q t) -> m j t q", t=PACK), ACT.Square)
-            nc.scalar.activation(part, part, ACT.Square, bias=1.0)
-            if k >= PACK:
-                nc.scalar.activation(part, part, ACT.Abs_reciprocal_sqrt)
-
-        z_mx = {}
-
-        dampings = {}
-
-        def invert(b, denom, lo, hi):
-            if lo % HALF == 0:
-                dampings[b, lo // HALF] = work.tile([P, HALF, PACK], F32, name="damping", tag="damping", bufs=2)
-            damping = dampings[b, lo // HALF]
-            for m in range(lo, hi, P):
-                back = psum.tile([P, PACK, P], F32, name="back", tag="turn", bufs=5)
-                for t in range(PACK):
-                    nc.tensor.transpose(back[:, t, :], denom[:, m // P, t, :], ident[:])
-                nc.scalar.activation(
-                    damping[:, m % HALF : m % HALF + P, :], back[:].rearrange("p t m -> p m t"), ACT.Abs_reciprocal_sqrt
+                    page[:].indirect(entries("sites", lo, hi)), feats[k][:, lo:hi], weights(k)[:, lo:hi], ALU.mult
                 )
 
-        def weigh(engine, b, z, lo, hi):
-            cols = slice(lo % HALF, lo % HALF + hi - lo)
-            engine.tensor_tensor(
-                z,
-                dampings[b, lo // HALF][:, cols, :].rearrange("p m t -> p (m t)"),
-                rate_il[b, lo // HALF][:, cols, :].rearrange("p m t -> p (m t)"),
+        origins = {}
+        targets = {}
+
+        def fetch_origins(k, tag, lo=0, hi=HOPS):
+            origins[k, lo] = sb([P, hi - lo], F32, "origin", tag=tag)
+            nc.vector.tensor_copy(origins[k, lo][:], pages[k % PAGES][:].indirect(entries("origins", lo, hi)))
+
+        def fetch_targets(k):
+            both = sb([P, HOPS], F32, "target", tag="got_w11" if k else "g2")
+            for lo in (0, HALF):
+                targets[k, lo] = both[:, lo : lo + HALF]
+                nc.vector.tensor_scalar(
+                    targets[k, lo],
+                    pages[k % PAGES][:].indirect(entries("targets", lo, lo + HALF)),
+                    -1.0,
+                    0.0,
+                    ALU.mult,
+                    ALU.add,
+                )
+
+        def fetch_difference(k, origin, part, lo, hi):
+            nc.vector.tensor_tensor(part, pages[k % PAGES][:].indirect(entries("targets", lo, hi)), origin, ALU.subtract)
+
+        def damp_tile():
+            return sb([P, HOPS], F32, "damp", bufs=2)
+
+        halves = [slice(lo, lo + HALF) for lo in range(0, HOPS, HALF)]
+        damps = {}
+
+        def differ(k):
+            damps[k] = damp_tile()
+            for half in halves:
+                diff = ring([P, HALF], "diff")
+                for m in range(0, HALF, P):
+                    cols = slice(half.start + m, half.start + m + P)
+                    pair = (targets[k, half.start][:, m : m + P], origins[k, 0][:, cols])
+                    for i, side in enumerate(pair):
+                        nc.tensor.matmul(diff[:, m : m + P], side, ident[:], start=i == 0, stop=i == 1, is_transpose=True)
+                nc.scalar.activation(damps[k][:, half], diff[:], ACT.Square)
+            for half in halves:
+                nc.scalar.activation(damps[k][:, half], damps[k][:, half], ACT.Square, bias=1.0)
+
+        def weigh_turned(k):
+            damp = sb([P, HOPS], F32, "damp0", tag="got_sc") if k == 0 else damps[k]
+            nc.scalar.activation(damp[:], damps[k][:], ACT.Abs_reciprocal_sqrt)
+            nc.gpsimd.tensor_tensor(
+                z0_turned[:, :, P * k : P * (k + 1)],
+                damp[:].rearrange("m (j r) -> m j r", r=P),
+                rate0[k][:].rearrange("m (j r) -> m j r", r=P),
                 ALU.mult,
             )
 
-        def quantise_z(b, z, codes, lo, hi):
-            scales = keep.tile([P, hi - lo], U8, name=f"z_sc{b}_{lo}", align_bytes=64)
-            nc.vector.quantize_mx(out=codes.bitcast(FP8X4), scales=scales[:], in_=z)
+        def weigh_slot(k, damp, diff, cuts):
+            for half in halves:
+                nc.scalar.activation(damp[:, half], diff[:, half], ACT.Square)
+            for half in halves:
+                nc.scalar.activation(damp[:, half], damp[:, half], ACT.Square, bias=1.0)
+            for half in halves:
+                nc.scalar.activation(damp[:, half], damp[:, half], ACT.Abs_reciprocal_sqrt)
+            for cols in cuts:
+                nc.gpsimd.tensor_tensor(z1[:, cols, k - PACK], damp[:, cols], rate1[k - PACK][:, cols], ALU.mult)
+
+        def slot_difference(k, tag):
+            diff = sb([P, HOPS], F32, "diff", tag=tag)
+            fetch_difference(k, origins[k, 0][:], diff[:], 0, HOPS)
+            return diff
+
+        z_mx = {}
+
+        def quantise_z(b, z, lo, hi, codes):
+            scales = sb([P, hi - lo], U8, f"z_sc{b}_{lo}")
+            nc.vector.quantize_mx(
+                out=codes.bitcast(FP8X4), scales=scales[:], in_=z.rearrange("p m t -> p (m t)")
+            )
             for m in range(lo, hi, P):
                 z_mx[b, m] = (codes[:, m - lo : m - lo + P], scales[:, m - lo : m - lo + P])
 
-        def score(m0, on_vector):
-            acc = psum.tile([P, NT, P], F32, name="acc2", tag="acc", bufs=3)
-            for n in range(NT):
-                for a in reversed(range(PASSES)):
-                    codes, scales = z_mx[a, m0]
-                    nc.tensor.matmul_mx(
-                        out=acc[:, n, :],
-                        lhsT=w4_w[:, a, 2 * P * n : 2 * P * (n + 1)].bitcast(FP4X4),
-                        lhsT_scale=w4_sc[:, a, P * n : P * (n + 1)],
-                        rhs=codes.bitcast(FP8X4),
-                        rhs_scale=scales,
-                        start=(a == PASSES - 1),
-                        stop=(a == 0),
-                    )
-            staged = work.tile([P, NT, P], F32, name="staged", tag="staged", bufs=8)
-            if on_vector:
-                nc.vector.tensor_copy(staged[:], acc[:])
-            else:
-                nc.scalar.copy(staged[:], acc[:])
-            nc.sync.dma_start(out.rearrange("(n p) m -> p n m", p=P)[:, :, m0 : m0 + P], staged[:])
+        sums = {}
 
-        def whole_block(k, denom):
-            page = place(k)
-            origin = origin_tile("origin")
-            width = HALF if k == BLOCKS - 1 else HOPS
+        def add_pass(a, m0):
+            if a == 0:
+                if m0 < 6 * P:
+                    sums[m0] = psum.tile([P, NT, P], F32, name="acc2", tag="acc", bufs=6)
+                else:
+                    sums[m0] = ring([P, NT, P], "acc2")
+            codes, scales = z_mx[a, m0]
+            for n in range(NT):
+                nc.tensor.matmul_mx(
+                    out=sums[m0][:, n, :],
+                    lhsT=w4_w[:, a, 2 * P * n : 2 * P * (n + 1)].bitcast(FP4X4),
+                    lhsT_scale=w4_sc[:, a, P * n : P * (n + 1)],
+                    rhs=codes.bitcast(FP8X4),
+                    rhs_scale=scales,
+                    start=(a == 0 and n == 0),
+                    stop=(a == PASSES - 1 and n == NT - 1),
+                )
+
+        def score(lo, hi):
+            staged = sb([P, NT, hi - lo], F32, f"staged{lo}")
+            for m0 in range(lo, hi, P):
+                add_pass(1, m0)
+                part = staged[:, :, m0 - lo : m0 - lo + P]
+                if m0 + P == HOPS:
+                    nc.vector.tensor_copy(part, sums[m0][:])
+                else:
+                    nc.scalar.copy(part, sums[m0][:])
+            nc.sync.dma_start(out.rearrange("(n p) m -> p n m", p=P)[:, :, lo:hi], staged[:])
+
+        def turn_rate(k):
             for lo in range(0, HOPS, HALF):
-                if lo % width == 0:
-                    fetch_origins(page, origin, lo, lo + width)
-                differ(k, denom, origin[:, lo : lo + HALF], fetch_targets(page, lo)[:], lo, lo + HALF)
+                turn = ring([P, HALF], "rate_turn")
+                for m in range(0, HALF, P):
+                    nc.tensor.transpose(turn[:, m : m + P], rate0[k][:, lo + m : lo + m + P], ident[:])
+                nc.scalar.copy(rate0[k][:, lo : lo + HALF], turn[:])
+
+        z0 = sb([P, HOPS, PACK], BF16, "z0")
+        z1 = sb([P, HOPS, PACK], BF16, "z1")
+
+        def turn_back():
+            for j0 in range(0, HOPS // P, 2):
+                bank = ring([P, 2, 2, P], "words")
+                for j in range(2):
+                    words = z0_turned[:, j0 + j, :].bitcast(F32)
+                    for u in range(2):
+                        nc.tensor.transpose(bank[:, j, u, :], words[:, u : KP // 2 : 2], ident[:])
+                nc.scalar.copy(
+                    z0[:, P * j0 : P * (j0 + 2), :].bitcast(F32).rearrange("p (j m) u -> p j m u", m=P),
+                    bank[:].rearrange("p j u m -> p j m u"),
+                )
 
         features(0)
-        quantise_w1(1, 0, "grouped", 1)
-        quantise_w1(1, 1, "origin", 1)
-        for k in range(1, PACK):
-            features(k)
-
-        denoms = [work.tile([P, HOPS // P, PACK, P], F32, name="denom", tag="denom", bufs=2) for b in range(PASSES)]
-        whole_block(0, denoms[0])
-        quantise_w1(2, 0, "grouped", 1)
-        quantise_w1(2, 1, "origin", 1)
+        place(0)
+        quantise_w1("g1", raw_mid, 1, 1, 0, False)
+        quantise_w1("g2", raw_mid, 2, 2, P, False)
+        quantise_w1("g4", raw_end, PACK, PACK, 0, True)
+        features(1)
+        fetch_origins(0, "g1")
+        fetch_targets(0)
+        place(1)
+        features(2)
+        features(3)
+        turn_rate(0)
+        differ(0)
         for k in range(PACK, BLOCKS):
             features(k)
+        origin_tags = ("g4_codes", "got_w0")
+        place(2)
+        fetch_origins(1, origin_tags[1])
+        fetch_targets(1)
+        fetch_origins(2, origin_tags[0])
+        preweigh(5, "raw128_1")
+        z0_turned = sb([P, HOPS // P, KP], BF16, "z0_turned")
+        weigh_turned(0)
+        for k in range(1, PACK):
+            turn_rate(k)
+            differ(k)
+            weigh_turned(k)
+            place(k + 2)
+            if k + 1 < PACK:
+                fetch_targets(k + 1)
+                fetch_origins(k + 2, origin_tags[k % 2])
+            if k == 2:
+                preweigh(6, "rate0_2")
 
-        rate_il = {}
-        for b in range(PASSES):
-            for i in range(2):
-                raw = load_rows(rate, b, HALF * i, HALF * (i + 1), "raw", 3)
-                woven = work.tile([P, HALF, PACK], F32, name="rate_il", tag="wide", bufs=4, align_bytes=64)
-                nc.scalar.copy(woven[:], raw[:].rearrange("p t m -> p m t"))
-                rate_il[b, i] = woven
+        whole = [slice(0, HOPS)]
+        diff4 = slot_difference(4, "raw128_0")
+        fetch_origins(5, feats_tag(5))
+        diff5 = slot_difference(5, "g1")
+        weigh_slot(4, damps[3], diff4, whole)
+        damp5 = sb([P, HOPS], F32, "damp5", tag="raw128_0")
+        weigh_slot(5, damp5, diff5, whole)
+        preweigh(LAST, "rate1_1")
+        turn_back()
+        place(6)
+        fetch_origins(6, feats_tag(6))
+        diff6 = slot_difference(6, "g2")
+        weigh_slot(6, damp5, diff6, halves)
+        codes0 = sb([P, HOPS], U32, "codes0", tag=feats_tag(LAST))
+        quantise_z(0, z0[:], 0, HOPS, codes0[:])
+        place(LAST)
 
+        def invert(part, diff):
+            nc.scalar.activation(part, diff, ACT.Square)
+            nc.scalar.activation(part, part, ACT.Square, bias=1.0)
+            nc.scalar.activation(part, part, ACT.Abs_reciprocal_sqrt)
 
-        def block_and_inverse(k):
-            b = k // PACK
-            last = k == BLOCKS - 1
-            page = place(k)
-            origin = origin_tile("last_origin" if last else "origin")
-            width = CHUNK if last else HOPS
-            for lo in range(0, HOPS, HALF):
-                target = fetch_targets(page, lo)
-                for m in range(lo, lo + HALF, min(width, HALF)):
-                    if m % width == 0:
-                        fetch_origins(page, origin, m, m + width)
-                    hi = m + min(width, HALF)
-                    differ(k, denoms[b], origin[:, m:hi], target[:, m - lo : hi - lo], m, hi)
-                    if k == PACK - 1:
-                        invert(b, denoms[b], m, hi)
-
-        z0 = []
-        for k in range(1, BLOCKS):
-            block_and_inverse(k)
-            if k >= BLOCKS - 2:
-                lo = HALF * len(z0)
-                z0.append(keep.tile([P, HALF * PACK], BF16, name="z0", tag=f"feats{k}", align_bytes=64))
-                weigh(nc.gpsimd, 0, z0[-1][:], lo, lo + HALF)
-
-        codes0 = work.tile([P, HOPS], U32, name="codes0", tag="page0", bufs=1, align_bytes=64)
-        for lo in range(0, HOPS, HALF):
-            quantise_z(0, z0[lo // HALF][:], codes0[:, lo : lo + HALF], lo, lo + HALF)
-        for lo, hi in ((0, 256), (256, 512), (512, 768), (768, 896), (896, 1024)):
-            z1 = work.tile([P, hi - lo, PACK], BF16, name="z1", tag="z1", bufs=2, align_bytes=64)
-            for m in range(lo, hi, P):
-                back = psum.tile([P, PACK, P], F32, name="back", tag="turn", bufs=5)
-                for t in range(PACK):
-                    nc.tensor.transpose(back[:, t, :], denoms[1][:, m // P, t, :], ident[:])
-                nc.vector.tensor_tensor(
-                    z1[:, m - lo : m - lo + P, :],
-                    back[:].rearrange("p t m -> p m t"),
-                    rate_il[1, m // HALF][:, m % HALF : m % HALF + P, :],
-                    ALU.mult,
-                )
-            codes1 = keep.tile([P, hi - lo], U32, name=f"codes1_{lo}", align_bytes=64)
-            quantise_z(1, z1[:].rearrange("p m t -> p (m t)"), codes1[:], lo, hi)
+        for i in range(2):
+            fetch_origins(LAST, feats_tag(PACK + i), HALF * i, HALF * (i + 1))
         for m0 in range(0, HOPS, P):
-            score(m0, m0 + P == HOPS)
+            add_pass(0, m0)
+
+        diff = sb([P, HOPS], F32, "diff", tag="rate1_2")
+        for lo, hi in TAIL_CUTS:
+            fetch_difference(LAST, origins[LAST, lo - lo % HALF][:, lo % HALF : lo % HALF + hi - lo], diff[:, lo:hi], lo, hi)
+            invert(diff[:, lo:hi], diff[:, lo:hi])
+        for lo, hi in TAIL_CUTS:
+            nc.vector.tensor_tensor(z1[:, lo:hi, PACK - 1], diff[:, lo:hi], rate1[PACK - 1][:, lo:hi], ALU.mult)
+            quantise_z(1, z1[:, lo:hi, :], lo, hi, sb([P, hi - lo], U32, f"codes1_{lo}")[:])
+        for lo, hi in TAIL_CUTS:
+            score(lo, hi)

@@ -27,6 +27,7 @@ QUAD = P // PACK
 BLOCKS = H // P
 LAST = BLOCKS - 1
 PAGES = 2
+HEAD_CUTS = ((0, 256), (256, 512), (512, 1024))
 TAIL_CUTS = ((0, 256), (256, 512), (512, 768), (768, 896), (896, 1024))
 
 
@@ -58,12 +59,12 @@ def tile_list_vacancy_hop_barriers_kernel(
             rows = slice(32 * q, 32 * q + 8)
             nc.sync.dma_start(landed_sc[rows, :].bitcast(I32), tab_scales[:, 4 * q : 4 * q + 4, :].bitcast(I32))
             nc.vector.tensor_copy(tab_sc[rows, :].bitcast(I32), landed_sc[rows, :].bitcast(I32))
-        pages = [sb([P, T2], F32, "page0")]
-        nc.vector.memset(pages[0][:], 0.0)
+        pages = [sb([P, T2], F32, "page0", tag="landed_sc")]
+        nc.gpsimd.memset(pages[0][:], 0.0)
         ident = sb([P, P], F32, "ident")
         make_identity(nc, ident[:])
 
-        tab_w = [sb([P, T], U32, "tab_w0", tag="page1"), sb([P, T], U32, "tab_w1", tag="z0_turned")]
+        tab_w = [sb([P, T], U32, "tab_w0", tag="z0_turned"), sb([P, T], U32, "tab_w1", tag="page1")]
 
         def load_tab(a):
             nc.sync.dma_start(tab_w[a][:].bitcast(I32), tab_words[a].rearrange("p t i -> p (t i)").bitcast(I32))
@@ -97,7 +98,7 @@ def tile_list_vacancy_hop_barriers_kernel(
         w4_w = sb([P, PASSES, 2 * N], U8, "w4_w")
         nc.sync.dma_start(w4_w[:].bitcast(I32), w4_words.rearrange("a p n -> p a n").bitcast(I32))
         w4_sc = sb([P, PASSES, N], U8, "w4_sc")
-        nc.vector.memset(w4_sc[:].rearrange("p a n -> p (a n)").bitcast(I32), 0)
+        nc.gpsimd.memset(w4_sc[:].rearrange("p a n -> p (a n)").bitcast(I32), 0)
         for q in range(4):
             nc.sync.dma_start(
                 w4_sc[32 * q : 32 * q + 4, :, :].bitcast(I32),
@@ -138,9 +139,9 @@ def tile_list_vacancy_hop_barriers_kernel(
 
         quantise_w1("g0", raw_head, 0, 1, 0, False)
 
-        got_w1 = [sb([P, HALF], U32, f"got_w1{i}") for i in range(2)]
-        for i in range(2):
-            nc.vector.tensor_copy(got_w1[i][:], tab_w[1][:].indirect(entries("ions", HALF * i, HALF * (i + 1))))
+        got_w1 = sb([P, S], U32, "got_w1")
+        for lo, hi in HEAD_CUTS:
+            nc.vector.tensor_copy(got_w1[:, lo:hi], tab_w[1][:].indirect(entries("ions", lo, hi)))
 
         pages.append(sb([P, T2], F32, "page1"))
         nc.gpsimd.memset(pages[1][:], 0.0)
@@ -155,17 +156,16 @@ def tile_list_vacancy_hop_barriers_kernel(
 
         def features(k):
             feats[k] = sb([P, S], F32, f"feats{k}", tag=feats_tag(k))
-            for i in range(2):
-                cols = slice(HALF * i, HALF * (i + 1))
-                acc = ring([P, HALF], "acc1")
+            for lo, hi in HEAD_CUTS if k == 0 else ((0, HALF), (HALF, S)):
+                cols = slice(lo, hi)
+                acc = ring([P, hi - lo], "acc1")
                 for a in range(PASSES):
-                    moving = got_w0[:, cols] if a == 0 else got_w1[i][:]
                     codes, scales = w1_mx[k, a]
                     nc.tensor.matmul_mx(
                         out=acc[:],
                         lhsT=codes.bitcast(FP8X4),
                         lhsT_scale=scales,
-                        rhs=moving.bitcast(FP8X4),
+                        rhs=(got_w0, got_w1)[a][:, cols].bitcast(FP8X4),
                         rhs_scale=got_sc[4 * a : P, cols],
                         start=(a == 0),
                         stop=(a == PASSES - 1),
@@ -175,6 +175,9 @@ def tile_list_vacancy_hop_barriers_kernel(
         def weights(k):
             return site_w[:] if k < PACK else dealt_w[:, k - PACK, :]
 
+        def page_of(k):
+            return pages[min(k, LAST - 1) % PAGES]
+
         weighted = {}
 
         def preweigh(k, tag):
@@ -182,13 +185,12 @@ def tile_list_vacancy_hop_barriers_kernel(
             nc.gpsimd.tensor_tensor(weighted[k][:], feats[k][:], weights(k), ALU.mult)
 
         def place(k):
-            page = pages[k % PAGES]
+            page = page_of(k)
             if k in weighted:
                 nc.vector.tensor_copy(page[:].indirect(entries("sites", 0, S)), weighted[k][:])
                 return
-            width = HALF if k == 0 else S
-            for lo in range(0, S, width):
-                hi = lo + width
+            first = HEAD_CUTS[0][1]
+            for lo, hi in ((0, first), (first, S)) if k == 0 else ((0, S),):
                 nc.vector.tensor_tensor(
                     page[:].indirect(entries("sites", lo, hi)), feats[k][:, lo:hi], weights(k)[:, lo:hi], ALU.mult
                 )
@@ -198,15 +200,15 @@ def tile_list_vacancy_hop_barriers_kernel(
 
         def fetch_origins(k, tag, lo=0, hi=HOPS):
             origins[k, lo] = sb([P, hi - lo], F32, "origin", tag=tag)
-            nc.vector.tensor_copy(origins[k, lo][:], pages[k % PAGES][:].indirect(entries("origins", lo, hi)))
+            nc.vector.tensor_copy(origins[k, lo][:], page_of(k)[:].indirect(entries("origins", lo, hi)))
 
         def fetch_targets(k):
-            both = sb([P, HOPS], F32, "target", tag="got_w11" if k else "g2")
+            both = sb([P, HOPS], F32, "target", tag="got_w1" if k else "g2")
             for lo in (0, HALF):
                 targets[k, lo] = both[:, lo : lo + HALF]
                 nc.vector.tensor_scalar(
                     targets[k, lo],
-                    pages[k % PAGES][:].indirect(entries("targets", lo, lo + HALF)),
+                    page_of(k)[:].indirect(entries("targets", lo, lo + HALF)),
                     -1.0,
                     0.0,
                     ALU.mult,
@@ -214,7 +216,7 @@ def tile_list_vacancy_hop_barriers_kernel(
                 )
 
         def fetch_difference(k, origin, part, lo, hi):
-            nc.vector.tensor_tensor(part, pages[k % PAGES][:].indirect(entries("targets", lo, hi)), origin, ALU.subtract)
+            nc.vector.tensor_tensor(part, page_of(k)[:].indirect(entries("targets", lo, hi)), origin, ALU.subtract)
 
         def damp_tile():
             return sb([P, HOPS], F32, "damp", bufs=2)
@@ -349,6 +351,8 @@ def tile_list_vacancy_hop_barriers_kernel(
         for k in range(1, PACK):
             turn_rate(k)
             differ(k)
+            if k == PACK - 1:
+                preweigh(LAST, feats_tag(LAST - 1))
             weigh_turned(k)
             place(k + 2)
             if k + 1 < PACK:
@@ -364,13 +368,12 @@ def tile_list_vacancy_hop_barriers_kernel(
         weigh_slot(4, damps[3], diff4, whole)
         damp5 = sb([P, HOPS], F32, "damp5", tag="raw128_0")
         weigh_slot(5, damp5, diff5, whole)
-        preweigh(LAST, "rate1_1")
         turn_back()
         place(6)
-        fetch_origins(6, feats_tag(6))
-        diff6 = slot_difference(6, "g2")
-        weigh_slot(6, damp5, diff6, halves)
-        codes0 = sb([P, HOPS], U32, "codes0", tag=feats_tag(LAST))
+        fetch_origins(6, "g2")
+        diff6 = slot_difference(6, "rate1_1")
+        weigh_slot(6, diff6, diff6, halves)
+        codes0 = sb([P, HOPS], U32, "codes0", tag="raw128_0")
         quantise_z(0, z0[:], 0, HOPS, codes0[:])
         place(LAST)
 
@@ -379,17 +382,20 @@ def tile_list_vacancy_hop_barriers_kernel(
             nc.scalar.activation(part, part, ACT.Square, bias=1.0)
             nc.scalar.activation(part, part, ACT.Abs_reciprocal_sqrt)
 
-        for i in range(2):
-            fetch_origins(LAST, feats_tag(PACK + i), HALF * i, HALF * (i + 1))
         for m0 in range(0, HOPS, P):
             add_pass(0, m0)
 
+        for i in range(2):
+            fetch_origins(LAST, feats_tag(PACK + i), HALF * i, HALF * (i + 1))
         diff = sb([P, HOPS], F32, "diff", tag="rate1_2")
         for lo, hi in TAIL_CUTS:
-            fetch_difference(LAST, origins[LAST, lo - lo % HALF][:, lo % HALF : lo % HALF + hi - lo], diff[:, lo:hi], lo, hi)
+            origin = origins[LAST, lo - lo % HALF][:, lo % HALF : lo % HALF + hi - lo]
+            fetch_difference(LAST, origin, diff[:, lo:hi], lo, hi)
             invert(diff[:, lo:hi], diff[:, lo:hi])
-        for lo, hi in TAIL_CUTS:
-            nc.vector.tensor_tensor(z1[:, lo:hi, PACK - 1], diff[:, lo:hi], rate1[PACK - 1][:, lo:hi], ALU.mult)
-            quantise_z(1, z1[:, lo:hi, :], lo, hi, sb([P, hi - lo], U32, f"codes1_{lo}")[:])
-        for lo, hi in TAIL_CUTS:
-            score(lo, hi)
+        for m0 in range(0, HOPS + P, P):
+            if m0 < HOPS:
+                cols = slice(m0, m0 + P)
+                nc.vector.tensor_tensor(z1[:, cols, PACK - 1], diff[:, cols], rate1[PACK - 1][:, cols], ALU.mult)
+            if m0 > 0:
+                quantise_z(1, z1[:, m0 - P : m0, :], m0 - P, m0, sb([P, P], U32, f"codes1_{m0}")[:])
+                score(m0 - P, m0)

@@ -198,12 +198,14 @@ def tile_list_vacancy_hop_barriers_kernel(
         origins = {}
         targets = {}
 
-        def fetch_origins(k, tag, lo=0, hi=HOPS):
-            origins[k, lo] = sb([P, hi - lo], F32, "origin", tag=tag)
-            nc.vector.tensor_copy(origins[k, lo][:], page_of(k)[:].indirect(entries("origins", lo, hi)))
+        def row(tag, width=HOPS):
+            return sb([P, width], F32, "row", tag=tag)[:]
 
-        def fetch_targets(k):
-            both = sb([P, HOPS], F32, "target", tag="got_w1" if k else "g2")
+        def fetch_origins(k, into, lo=0, hi=HOPS):
+            origins[k, lo] = into
+            nc.vector.tensor_copy(into, page_of(k)[:].indirect(entries("origins", lo, hi)))
+
+        def fetch_targets(k, both):
             for lo in (0, HALF):
                 targets[k, lo] = both[:, lo : lo + HALF]
                 nc.vector.tensor_scalar(
@@ -234,7 +236,6 @@ def tile_list_vacancy_hop_barriers_kernel(
                     for i, side in enumerate(pair):
                         nc.tensor.matmul(diff[:, m : m + P], side, ident[:], start=i == 0, stop=i == 1, is_transpose=True)
                 nc.scalar.activation(damps[k][:, half], diff[:], ACT.Square)
-            for half in halves:
                 nc.scalar.activation(damps[k][:, half], damps[k][:, half], ACT.Square, bias=1.0)
 
         def weigh_turned(k):
@@ -247,20 +248,14 @@ def tile_list_vacancy_hop_barriers_kernel(
                 ALU.mult,
             )
 
-        def weigh_slot(k, damp, diff, cuts):
+        def weigh_slot(k):
+            damp = damps[k]
             for half in halves:
-                nc.scalar.activation(damp[:, half], diff[:, half], ACT.Square)
-            for half in halves:
-                nc.scalar.activation(damp[:, half], damp[:, half], ACT.Square, bias=1.0)
-            for half in halves:
-                nc.scalar.activation(damp[:, half], damp[:, half], ACT.Abs_reciprocal_sqrt)
-            for cols in cuts:
-                nc.gpsimd.tensor_tensor(z1[:, cols, k - PACK], damp[:, cols], rate1[k - PACK][:, cols], ALU.mult)
-
-        def slot_difference(k, tag):
-            diff = sb([P, HOPS], F32, "diff", tag=tag)
-            fetch_difference(k, origins[k, 0][:], diff[:], 0, HOPS)
-            return diff
+                back = ring([P, HALF], "back")
+                for m in range(0, HALF, P):
+                    nc.tensor.transpose(back[:, m : m + P], damp[:, half.start + m : half.start + m + P], ident[:])
+                nc.scalar.activation(damp[:, half], back[:], ACT.Abs_reciprocal_sqrt)
+                nc.gpsimd.tensor_tensor(z1[:, half, k - PACK], damp[:, half], rate1[k - PACK][:, half], ALU.mult)
 
         z_mx = {}
 
@@ -331,8 +326,8 @@ def tile_list_vacancy_hop_barriers_kernel(
         quantise_w1("g2", raw_mid, 2, 2, P, False)
         quantise_w1("g4", raw_end, PACK, PACK, 0, True)
         features(1)
-        fetch_origins(0, "g1")
-        fetch_targets(0)
+        fetch_origins(0, row("g1"))
+        fetch_targets(0, row("g2"))
         place(1)
         features(2)
         features(3)
@@ -342,39 +337,37 @@ def tile_list_vacancy_hop_barriers_kernel(
             features(k)
         origin_tags = ("g4_codes", "got_w0")
         place(2)
-        fetch_origins(1, origin_tags[1])
-        fetch_targets(1)
-        fetch_origins(2, origin_tags[0])
+        fetch_origins(1, row(origin_tags[1]))
+        fetch_targets(1, row("got_w1"))
+        fetch_origins(2, row(origin_tags[0]))
         preweigh(5, "raw128_1")
         z0_turned = sb([P, HOPS // P, KP], BF16, "z0_turned")
         weigh_turned(0)
-        for k in range(1, PACK):
-            turn_rate(k)
+        for k in range(1, LAST):
+            if k < PACK:
+                turn_rate(k)
+            if k == PACK:
+                turn_back()
             differ(k)
+            if k < PACK:
+                weigh_turned(k)
+            else:
+                weigh_slot(k)
+            if k in (2, 3):
+                preweigh(k + PACK, f"rate0_{k}")
+            if k < PACK:
+                place(k + 2)
+                fetch_targets(k + 1, row("got_w1"))
+            if k < PACK - 1:
+                fetch_origins(k + 2, row(origin_tags[k % 2]))
             if k == PACK - 1:
-                preweigh(LAST, feats_tag(LAST - 1))
-            weigh_turned(k)
-            place(k + 2)
-            if k + 1 < PACK:
-                fetch_targets(k + 1)
-                fetch_origins(k + 2, origin_tags[k % 2])
-            if k == 2:
-                preweigh(6, "rate0_2")
-
-        whole = [slice(0, HOPS)]
-        diff4 = slot_difference(4, "raw128_0")
-        fetch_origins(5, feats_tag(5))
-        diff5 = slot_difference(5, "g1")
-        weigh_slot(4, damps[3], diff4, whole)
-        damp5 = sb([P, HOPS], F32, "damp5", tag="raw128_0")
-        weigh_slot(5, damp5, diff5, whole)
-        turn_back()
-        place(6)
-        fetch_origins(6, "g2")
-        diff6 = slot_difference(6, "rate1_1")
-        weigh_slot(6, diff6, diff6, halves)
-        codes0 = sb([P, HOPS], U32, "codes0", tag="raw128_0")
-        quantise_z(0, z0[:], 0, HOPS, codes0[:])
+                both = row(origin_tags[k % 2], 2 * HOPS)
+                fetch_origins(k + 2, both[:, 0:HOPS])
+                fetch_targets(k + 2, both[:, HOPS : 2 * HOPS])
+                place(k + 3)
+                fetch_origins(k + 3, row("g2"))
+            if k == PACK:
+                fetch_targets(k + 2, row("got_w1"))
         place(LAST)
 
         def invert(part, diff):
@@ -382,12 +375,13 @@ def tile_list_vacancy_hop_barriers_kernel(
             nc.scalar.activation(part, part, ACT.Square, bias=1.0)
             nc.scalar.activation(part, part, ACT.Abs_reciprocal_sqrt)
 
+        for i in range(2):
+            fetch_origins(LAST, row(feats_tag(PACK + i), HALF), HALF * i, HALF * (i + 1))
+        codes0 = sb([P, HOPS], U32, "codes0", tag="rate1_2")
+        quantise_z(0, z0[:], 0, HOPS, codes0[:])
         for m0 in range(0, HOPS, P):
             add_pass(0, m0)
-
-        for i in range(2):
-            fetch_origins(LAST, feats_tag(PACK + i), HALF * i, HALF * (i + 1))
-        diff = sb([P, HOPS], F32, "diff", tag="rate1_2")
+        diff = sb([P, HOPS], F32, "diff", tag="z0")
         for lo, hi in TAIL_CUTS:
             origin = origins[LAST, lo - lo % HALF][:, lo % HALF : lo % HALF + hi - lo]
             fetch_difference(LAST, origin, diff[:, lo:hi], lo, hi)

@@ -28,7 +28,7 @@ BLOCKS = H // P
 LAST = BLOCKS - 1
 PAGES = 2
 HEAD_CUTS = ((0, 256), (256, 512), (512, 1024))
-TAIL_CUTS = ((0, 256), (256, 512), (512, 768), (768, 896), (896, 1024))
+QUARTER = 256
 
 
 def tile_list_vacancy_hop_barriers_kernel(
@@ -91,9 +91,12 @@ def tile_list_vacancy_hop_barriers_kernel(
         dealt_w = sb([P, PACK, S], F32, "dealt_w")
         for q in range(PACK):
             nc.sync.dma_start(dealt_w[QUAD * q : QUAD * (q + 1), :, :], wgs.rearrange("(q t) j -> q t j", t=PACK))
-        rate1 = [sb([P, HOPS], F32, f"rate1_{t}") for t in range(PACK)]
+        ending = sb([P, 3 * HOPS], F32, "ending")
+        rate1 = [sb([P, HOPS], F32, f"rate1_{t}")[:] for t in range(2)]
+        rate1 = rate1 + [ending[:, 2 * HOPS : 3 * HOPS], ending[:, HOPS : 2 * HOPS]]
+        rate_rows = rate[KP:H, :].rearrange("(p t) m -> p t m", t=PACK)
         for t in range(PACK):
-            nc.sync.dma_start(rate1[t][:], rate[KP:H, :].rearrange("(p t) m -> p t m", t=PACK)[:, t, :])
+            nc.sync.dma_start(rate1[t], rate_rows[:, t, :])
 
         w4_w = sb([P, PASSES, 2 * N], U8, "w4_w")
         nc.sync.dma_start(w4_w[:].bitcast(I32), w4_words.rearrange("a p n -> p a n").bitcast(I32))
@@ -112,32 +115,33 @@ def tile_list_vacancy_hop_barriers_kernel(
 
         w1_mx = {}
 
-        def quantise_w1(name, raws, first, blocks, c0, dealt):
+        def quantise_w1(name, raws, first, blocks, c0, tag=None):
             width = P * blocks
-            grouped = sb([P, PASSES, width, PACK], BF16, name)
-            for a in range(PASSES):
+            passes = sorted(raws)
+            grouped = sb([P, len(passes), width, PACK], BF16, name, tag=tag)
+            for i, a in enumerate(passes):
                 src = raws[a][:, :, c0 : c0 + width]
-                if dealt:
+                if first >= PACK:
                     nc.scalar.copy(
-                        grouped[:, a].rearrange("p (t m) j -> p m t j", t=PACK),
+                        grouped[:, i].rearrange("p (t m) j -> p m t j", t=PACK),
                         src.rearrange("p j (m t) -> p m t j", t=PACK),
                     )
                 else:
                     nc.scalar.copy(
-                        grouped[:, a].rearrange("p (c i) j -> p c j i", i=PACK),
+                        grouped[:, i].rearrange("p (c i) j -> p c j i", i=PACK),
                         src.rearrange("p j (c i) -> p c j i", i=PACK),
                     )
-            codes = sb([P, PASSES * width], U32, name + "_codes")
-            scales = sb([P, PASSES * width], U8, name + "_sc")
+            codes = sb([P, len(passes) * width], U32, name + "_codes")
+            scales = sb([P, len(passes) * width], U8, name + "_sc")
             nc.vector.quantize_mx(
                 out=codes[:].bitcast(FP8X4), scales=scales[:], in_=grouped[:].rearrange("p a c j -> p (a c j)")
             )
-            for a in range(PASSES):
+            for i, a in enumerate(passes):
                 for b in range(blocks):
-                    cols = slice(width * a + P * b, width * a + P * (b + 1))
+                    cols = slice(width * i + P * b, width * i + P * (b + 1))
                     w1_mx[first + b, a] = (codes[:, cols], scales[:, cols])
 
-        quantise_w1("g0", raw_head, 0, 1, 0, False)
+        quantise_w1("g0", dict(enumerate(raw_head)), 0, 1, 0)
 
         got_w1 = sb([P, S], U32, "got_w1")
         for lo, hi in HEAD_CUTS:
@@ -239,8 +243,8 @@ def tile_list_vacancy_hop_barriers_kernel(
                 nc.scalar.activation(damps[k][:, half], damps[k][:, half], ACT.Square, bias=1.0)
 
         def weigh_turned(k):
-            damp = sb([P, HOPS], F32, "damp0", tag="got_sc") if k == 0 else damps[k]
-            nc.scalar.activation(damp[:], damps[k][:], ACT.Abs_reciprocal_sqrt)
+            damp = damps[k]
+            nc.scalar.activation(damp[:], damp[:], ACT.Abs_reciprocal_sqrt)
             nc.gpsimd.tensor_tensor(
                 z0_turned[:, :, P * k : P * (k + 1)],
                 damp[:].rearrange("m (j r) -> m j r", r=P),
@@ -254,8 +258,12 @@ def tile_list_vacancy_hop_barriers_kernel(
                 back = ring([P, HALF], "back")
                 for m in range(0, HALF, P):
                     nc.tensor.transpose(back[:, m : m + P], damp[:, half.start + m : half.start + m + P], ident[:])
-                nc.scalar.activation(damp[:, half], back[:], ACT.Abs_reciprocal_sqrt)
-                nc.gpsimd.tensor_tensor(z1[:, half, k - PACK], damp[:, half], rate1[k - PACK][:, half], ALU.mult)
+                if k == LAST - 1:
+                    part = result = ending[:, half]
+                else:
+                    part, result = damp[:, half], z1[:, half, k - PACK]
+                nc.scalar.activation(part, back[:], ACT.Abs_reciprocal_sqrt)
+                nc.gpsimd.tensor_tensor(result, part, rate1[k - PACK][:, half], ALU.mult)
 
         z_mx = {}
 
@@ -322,29 +330,33 @@ def tile_list_vacancy_hop_barriers_kernel(
 
         features(0)
         place(0)
-        quantise_w1("g1", raw_mid, 1, 1, 0, False)
-        quantise_w1("g2", raw_mid, 2, 2, P, False)
-        quantise_w1("g4", raw_end, PACK, PACK, 0, True)
-        features(1)
+        quantise_w1("g1", dict(enumerate(raw_mid)), 1, 1, 0)
+        quantise_w1("g2", dict(enumerate(raw_mid)), 2, 2, P)
         fetch_origins(0, row("g1"))
         fetch_targets(0, row("g2"))
+        quantise_w1("g4", {0: raw_end[0]}, PACK, PACK, 0)
+        features(1)
         place(1)
+        quantise_w1("g5", {1: raw_end[1]}, PACK, PACK, 0, tag="g4")
         features(2)
         features(3)
         turn_rate(0)
-        differ(0)
+        turn_rate(1)
         for k in range(PACK, BLOCKS):
             features(k)
-        origin_tags = ("g4_codes", "got_w0")
+        differ(0)
+        origin_tags = ("g4", "g2_codes")
         place(2)
         fetch_origins(1, row(origin_tags[1]))
-        fetch_targets(1, row("got_w1"))
+        fetch_targets(1, row("g2_sc"))
         fetch_origins(2, row(origin_tags[0]))
+        preweigh(3, feats_tag(2))
+        preweigh(4, feats_tag(1))
         preweigh(5, "raw128_1")
         z0_turned = sb([P, HOPS // P, KP], BF16, "z0_turned")
         weigh_turned(0)
         for k in range(1, LAST):
-            if k < PACK:
+            if 1 < k < PACK:
                 turn_rate(k)
             if k == PACK:
                 turn_back()
@@ -357,7 +369,7 @@ def tile_list_vacancy_hop_barriers_kernel(
                 preweigh(k + PACK, f"rate0_{k}")
             if k < PACK:
                 place(k + 2)
-                fetch_targets(k + 1, row("got_w1"))
+                fetch_targets(k + 1, row("g2_sc"))
             if k < PACK - 1:
                 fetch_origins(k + 2, row(origin_tags[k % 2]))
             if k == PACK - 1:
@@ -367,7 +379,7 @@ def tile_list_vacancy_hop_barriers_kernel(
                 place(k + 3)
                 fetch_origins(k + 3, row("g2"))
             if k == PACK:
-                fetch_targets(k + 2, row("got_w1"))
+                fetch_targets(k + 2, row("g2_sc"))
         place(LAST)
 
         def invert(part, diff):
@@ -375,21 +387,58 @@ def tile_list_vacancy_hop_barriers_kernel(
             nc.scalar.activation(part, part, ACT.Square, bias=1.0)
             nc.scalar.activation(part, part, ACT.Abs_reciprocal_sqrt)
 
-        for i in range(2):
-            fetch_origins(LAST, row(feats_tag(PACK + i), HALF), HALF * i, HALF * (i + 1))
-        codes0 = sb([P, HOPS], U32, "codes0", tag="rate1_2")
-        quantise_z(0, z0[:], 0, HOPS, codes0[:])
-        for m0 in range(0, HOPS, P):
-            add_pass(0, m0)
-        diff = sb([P, HOPS], F32, "diff", tag="z0")
-        for lo, hi in TAIL_CUTS:
-            origin = origins[LAST, lo - lo % HALF][:, lo % HALF : lo % HALF + hi - lo]
-            fetch_difference(LAST, origin, diff[:, lo:hi], lo, hi)
-            invert(diff[:, lo:hi], diff[:, lo:hi])
-        for m0 in range(0, HOPS + P, P):
-            if m0 < HOPS:
-                cols = slice(m0, m0 + P)
-                nc.vector.tensor_tensor(z1[:, cols, PACK - 1], diff[:, cols], rate1[PACK - 1][:, cols], ALU.mult)
-            if m0 > 0:
-                quantise_z(1, z1[:, m0 - P : m0, :], m0 - P, m0, sb([P, P], U32, f"codes1_{m0}")[:])
-                score(m0 - P, m0)
+        quarters = ending[:].rearrange("p (q m) -> p q m", m=QUARTER)
+        home = (10, 11, 9, 4)
+
+        def slot3(lo, hi):
+            return quarters[:, home[lo // QUARTER], lo % QUARTER : lo % QUARTER + hi - lo]
+
+        def difference(lo, hi):
+            start = max(s for kk, s in origins if kk == LAST and s <= lo)
+            fetch_difference(LAST, origins[LAST, start][:, lo - start : hi - start], slot3(lo, hi), lo, hi)
+            invert(slot3(lo, hi), slot3(lo, hi))
+
+        def product(lo, hi):
+            nc.vector.tensor_tensor(slot3(lo, hi), slot3(lo, hi), rate1[PACK - 1][:, lo:hi], ALU.mult)
+
+        def weave(lo, hi):
+            q = lo // QUARTER
+            pair = quarters[:, q : home[q] + 1 : home[q] - q, lo % QUARTER : lo % QUARTER + hi - lo]
+            nc.vector.tensor_copy(z1[:, lo:hi, 2:PACK], pair.rearrange("p s m -> p m s"))
+
+        def pack(lo, hi):
+            quantise_z(1, z1[:, lo:hi, :], lo, hi, sb([P, hi - lo], U32, f"codes1_{lo}")[:])
+
+        def first_pass(q, tag):
+            lo, hi = HALF * q, HALF * (q + 1)
+            quantise_z(0, z0[:, lo:hi, :], lo, hi, sb([P, HALF], U32, "codes0", tag=tag)[:])
+            for m0 in range(lo, hi, P):
+                add_pass(0, m0)
+
+        fetch_origins(LAST, row(feats_tag(PACK), QUARTER), 0, QUARTER)
+        fetch_origins(LAST, row(feats_tag(PACK + 1), QUARTER), QUARTER, HALF)
+        difference(0, 256)
+        difference(256, 512)
+        fetch_origins(LAST, row(feats_tag(PACK), HALF), HALF, HOPS)
+        first_pass(0, feats_tag(PACK + 1))
+        difference(512, 768)
+        product(0, 256)
+        product(256, 512)
+        weave(0, 256)
+        difference(768, 896)
+        difference(896, 1024)
+        pack(0, 256)
+        weave(256, 512)
+        product(512, 768)
+        pack(256, 512)
+        first_pass(1, feats_tag(PACK))
+        weave(512, 768)
+        product(768, 896)
+        product(896, 1024)
+        pack(512, 768)
+        weave(768, 896)
+        weave(896, 1024)
+        pack(768, 896)
+        pack(896, 1024)
+        for lo, hi in ((0, 128), (128, 256), (256, 512), (512, 768), (768, 896), (896, 1024)):
+            score(lo, hi)

@@ -91,12 +91,16 @@ def tile_list_vacancy_hop_barriers_kernel(
         dealt_w = sb([P, PACK, S], F32, "dealt_w")
         for q in range(PACK):
             nc.sync.dma_start(dealt_w[QUAD * q : QUAD * (q + 1), :, :], wgs.rearrange("(q t) j -> q t j", t=PACK))
-        ending = sb([P, 3 * HOPS], F32, "ending")
-        rate1 = [sb([P, HOPS], F32, f"rate1_{t}")[:] for t in range(2)]
-        rate1 = rate1 + [ending[:, 2 * HOPS : 3 * HOPS], ending[:, HOPS : 2 * HOPS]]
         rate_rows = rate[KP:H, :].rearrange("(p t) m -> p t m", t=PACK)
-        for t in range(PACK):
-            nc.sync.dma_start(rate1[t], rate_rows[:, t, :])
+        ending = sb([P, 3 * HOPS], F32, "ending")
+        rate_cuts = {0: (0, HALF, HOPS), 1: (0, HALF, HOPS), 2: (0, HALF, HALF + QUARTER, HOPS)}
+        rate1 = {}
+        for t, cuts in rate_cuts.items():
+            for lo, hi in zip(cuts, cuts[1:]):
+                rate1[t, lo] = sb([P, hi - lo], F32, f"rate1_{t}_{lo}")
+                nc.sync.dma_start(rate1[t, lo][:], rate_rows[:, t, lo:hi])
+        rate_last = ending[:, HOPS : 2 * HOPS]
+        nc.sync.dma_start(rate_last, rate_rows[:, PACK - 1, :])
 
         w4_w = sb([P, PASSES, 2 * N], U8, "w4_w")
         nc.sync.dma_start(w4_w[:].bitcast(I32), w4_words.rearrange("a p n -> p a n").bitcast(I32))
@@ -115,33 +119,39 @@ def tile_list_vacancy_hop_barriers_kernel(
 
         w1_mx = {}
 
-        def quantise_w1(name, raws, first, blocks, c0, tag=None):
+        grouped = {}
+
+        def round_w1(name, raw, first, blocks, c0, i, count, tag=None):
             width = P * blocks
-            passes = sorted(raws)
-            grouped = sb([P, len(passes), width, PACK], BF16, name, tag=tag)
-            for i, a in enumerate(passes):
-                src = raws[a][:, :, c0 : c0 + width]
-                if first >= PACK:
-                    nc.scalar.copy(
-                        grouped[:, i].rearrange("p (t m) j -> p m t j", t=PACK),
-                        src.rearrange("p j (m t) -> p m t j", t=PACK),
-                    )
-                else:
-                    nc.scalar.copy(
-                        grouped[:, i].rearrange("p (c i) j -> p c j i", i=PACK),
-                        src.rearrange("p j (c i) -> p c j i", i=PACK),
-                    )
+            if name not in grouped:
+                grouped[name] = sb([P, count, width, PACK], BF16, name, tag=tag)
+            src = raw[:, :, c0 : c0 + width]
+            if first >= PACK:
+                nc.scalar.copy(
+                    grouped[name][:, i].rearrange("p (t m) j -> p m t j", t=PACK),
+                    src.rearrange("p j (m t) -> p m t j", t=PACK),
+                )
+            else:
+                nc.scalar.copy(
+                    grouped[name][:, i].rearrange("p (c i) j -> p c j i", i=PACK),
+                    src.rearrange("p j (c i) -> p c j i", i=PACK),
+                )
+
+        def pack_w1(name, first, blocks, passes):
+            width = P * blocks
             codes = sb([P, len(passes) * width], U32, name + "_codes")
             scales = sb([P, len(passes) * width], U8, name + "_sc")
             nc.vector.quantize_mx(
-                out=codes[:].bitcast(FP8X4), scales=scales[:], in_=grouped[:].rearrange("p a c j -> p (a c j)")
+                out=codes[:].bitcast(FP8X4), scales=scales[:], in_=grouped[name][:].rearrange("p a c j -> p (a c j)")
             )
             for i, a in enumerate(passes):
                 for b in range(blocks):
                     cols = slice(width * i + P * b, width * i + P * (b + 1))
                     w1_mx[first + b, a] = (codes[:, cols], scales[:, cols])
 
-        quantise_w1("g0", dict(enumerate(raw_head)), 0, 1, 0)
+        for a in range(PASSES):
+            round_w1("g0", raw_head[a], 0, 1, 0, a, PASSES)
+        pack_w1("g0", 0, 1, (0, 1))
 
         got_w1 = sb([P, S], U32, "got_w1")
         for lo, hi in HEAD_CUTS:
@@ -209,9 +219,9 @@ def tile_list_vacancy_hop_barriers_kernel(
             origins[k, lo] = into
             nc.vector.tensor_copy(into, page_of(k)[:].indirect(entries("origins", lo, hi)))
 
-        def fetch_targets(k, both):
-            for lo in (0, HALF):
-                targets[k, lo] = both[:, lo : lo + HALF]
+        def fetch_targets(k, both, first=0, end=HOPS):
+            for lo in range(first, end, HALF):
+                targets[k, lo] = both[:, lo - first : lo - first + HALF]
                 nc.vector.tensor_scalar(
                     targets[k, lo],
                     page_of(k)[:].indirect(entries("targets", lo, lo + HALF)),
@@ -236,7 +246,8 @@ def tile_list_vacancy_hop_barriers_kernel(
                 diff = ring([P, HALF], "diff")
                 for m in range(0, HALF, P):
                     cols = slice(half.start + m, half.start + m + P)
-                    pair = (targets[k, half.start][:, m : m + P], origins[k, 0][:, cols])
+                    origin = origins[k, half.start][:, m : m + P] if (k, half.start) in origins else origins[k, 0][:, cols]
+                    pair = (targets[k, half.start][:, m : m + P], origin)
                     for i, side in enumerate(pair):
                         nc.tensor.matmul(diff[:, m : m + P], side, ident[:], start=i == 0, stop=i == 1, is_transpose=True)
                 nc.scalar.activation(damps[k][:, half], diff[:], ACT.Square)
@@ -244,7 +255,8 @@ def tile_list_vacancy_hop_barriers_kernel(
 
         def weigh_turned(k):
             damp = damps[k]
-            nc.scalar.activation(damp[:], damp[:], ACT.Abs_reciprocal_sqrt)
+            for half in halves:
+                nc.scalar.activation(damp[:, half], damp[:, half], ACT.Abs_reciprocal_sqrt)
             nc.gpsimd.tensor_tensor(
                 z0_turned[:, :, P * k : P * (k + 1)],
                 damp[:].rearrange("m (j r) -> m j r", r=P),
@@ -258,12 +270,12 @@ def tile_list_vacancy_hop_barriers_kernel(
                 back = ring([P, HALF], "back")
                 for m in range(0, HALF, P):
                     nc.tensor.transpose(back[:, m : m + P], damp[:, half.start + m : half.start + m + P], ident[:])
-                if k == LAST - 1:
-                    part = result = ending[:, half]
-                else:
-                    part, result = damp[:, half], z1[:, half, k - PACK]
+                part = low[:, k - PACK, half]
                 nc.scalar.activation(part, back[:], ACT.Abs_reciprocal_sqrt)
-                nc.gpsimd.tensor_tensor(result, part, rate1[k - PACK][:, half], ALU.mult)
+                cuts = [c for c in rate_cuts[k - PACK] if half.start <= c <= half.stop]
+                for lo, hi in zip(cuts, cuts[1:]):
+                    piece = low[:, k - PACK, lo:hi]
+                    nc.gpsimd.tensor_tensor(piece, piece, rate1[k - PACK, lo][:], ALU.mult)
 
         z_mx = {}
 
@@ -313,8 +325,6 @@ def tile_list_vacancy_hop_barriers_kernel(
                     nc.tensor.transpose(turn[:, m : m + P], rate0[k][:, lo + m : lo + m + P], ident[:])
                 nc.scalar.copy(rate0[k][:, lo : lo + HALF], turn[:])
 
-        z0 = sb([P, HOPS, PACK], BF16, "z0")
-        z1 = sb([P, HOPS, PACK], BF16, "z1")
 
         def turn_back():
             for j0 in range(0, HOPS // P, 2):
@@ -324,20 +334,33 @@ def tile_list_vacancy_hop_barriers_kernel(
                     for u in range(2):
                         nc.tensor.transpose(bank[:, j, u, :], words[:, u : KP // 2 : 2], ident[:])
                 nc.scalar.copy(
-                    z0[:, P * j0 : P * (j0 + 2), :].bitcast(F32).rearrange("p (j m) u -> p j m u", m=P),
+                    z0[j0 // PACK][:, P * (j0 % PACK) : P * (j0 % PACK + 2), :].bitcast(F32).rearrange("p (j m) u -> p j m u", m=P),
                     bank[:].rearrange("p j u m -> p j m u"),
                 )
 
+        def first_pass(q, tag):
+            lo, hi = HALF * q, HALF * (q + 1)
+            quantise_z(0, z0[q][:], lo, hi, sb([P, HALF], U32, "codes0", tag=tag)[:])
+            for m0 in range(lo, hi, P):
+                add_pass(0, m0)
+
         features(0)
         place(0)
-        quantise_w1("g1", dict(enumerate(raw_mid)), 1, 1, 0)
-        quantise_w1("g2", dict(enumerate(raw_mid)), 2, 2, P)
-        fetch_origins(0, row("g1"))
-        fetch_targets(0, row("g2"))
-        quantise_w1("g4", {0: raw_end[0]}, PACK, PACK, 0)
+        round_w1("g1", raw_mid[0], 1, 1, 0, 0, PASSES)
+        for a in range(PASSES):
+            round_w1("g2", raw_mid[a], 2, 2, P, a, PASSES)
+        round_w1("g1", raw_mid[1], 1, 1, 0, 1, PASSES)
+        pack_w1("g2", 2, 2, (0, 1))
+        pack_w1("g1", 1, 1, (0, 1))
+        both = row("g2", 2 * HOPS)
+        fetch_origins(0, both[:, 0:HOPS])
+        fetch_targets(0, both[:, HOPS : 2 * HOPS])
+        round_w1("g4", raw_end[0], PACK, PACK, 0, 0, 1)
+        pack_w1("g4", PACK, PACK, (0,))
         features(1)
         place(1)
-        quantise_w1("g5", {1: raw_end[1]}, PACK, PACK, 0, tag="g4")
+        round_w1("g5", raw_end[1], PACK, PACK, 0, 0, 1, tag="g4")
+        pack_w1("g5", PACK, PACK, (1,))
         features(2)
         features(3)
         turn_rate(0)
@@ -355,31 +378,56 @@ def tile_list_vacancy_hop_barriers_kernel(
         preweigh(5, "raw128_1")
         z0_turned = sb([P, HOPS // P, KP], BF16, "z0_turned")
         weigh_turned(0)
-        for k in range(1, LAST):
-            if 1 < k < PACK:
+        z0 = [sb([P, HALF, PACK], BF16, "z0", tag=tag) for tag in ("got_w0", "g1")]
+        for k in range(1, PACK):
+            if k > 1:
                 turn_rate(k)
-            if k == PACK:
-                turn_back()
             differ(k)
-            if k < PACK:
-                weigh_turned(k)
-            else:
-                weigh_slot(k)
-            if k in (2, 3):
+            weigh_turned(k)
+            if k > 1:
                 preweigh(k + PACK, f"rate0_{k}")
-            if k < PACK:
-                place(k + 2)
-                fetch_targets(k + 1, row("g2_sc"))
+            place(k + 2)
+            target = row("g2_sc")
+            fetch_targets(k + 1, target[:, 0:HALF], 0, HALF)
+            if k == PACK - 1:
+                fetch_origins(k + 2, row(origin_tags[k % 2], 2 * HOPS)[:, 0:HOPS])
+            fetch_targets(k + 1, target[:, HALF:HOPS], HALF, HOPS)
             if k < PACK - 1:
                 fetch_origins(k + 2, row(origin_tags[k % 2]))
-            if k == PACK - 1:
-                both = row(origin_tags[k % 2], 2 * HOPS)
-                fetch_origins(k + 2, both[:, 0:HOPS])
-                fetch_targets(k + 2, both[:, HOPS : 2 * HOPS])
-                place(k + 3)
-                fetch_origins(k + 3, row("g2"))
-            if k == PACK:
-                fetch_targets(k + 2, row("g2_sc"))
+
+        def invert_halves(diff, result):
+            for half in halves:
+                nc.scalar.activation(diff[:, half], diff[:, half], ACT.Square)
+            for half in halves:
+                nc.scalar.activation(diff[:, half], diff[:, half], ACT.Square, bias=1.0)
+            for half in halves:
+                nc.scalar.activation(result[:, half], diff[:, half], ACT.Abs_reciprocal_sqrt)
+
+        def times_rate(k, result, values):
+            cuts = rate_cuts[k - PACK]
+            for lo, hi in zip(cuts, cuts[1:]):
+                nc.gpsimd.tensor_tensor(result[:, lo:hi], values[:, lo:hi], rate1[k - PACK, lo][:], ALU.mult)
+
+        diff5 = row("g2")
+        fetch_difference(5, origins[5, 0], diff5, 0, HOPS)
+        place(6)
+        for half in halves:
+            fetch_origins(6, row(feats_tag(PACK - 1 + half.start // HALF), HALF), half.start, half.stop)
+        differ(PACK)
+        low = sb([P, 2, HOPS], F32, "low", tag=origin_tags[1])
+        weigh_slot(PACK)
+        invert_halves(diff5, diff5)
+        times_rate(5, low[:, 1, :], diff5)
+        turn_back()
+        diff6 = row(f"rate1_1_{HALF}")
+        for half in halves:
+            fetch_difference(6, origins[6, half.start], diff6[:, half], half.start, half.stop)
+        first_pass(0, "g2")
+        invert_halves(diff6, ending)
+        times_rate(6, ending, ending)
+        z1 = sb([P, HOPS, PACK], BF16, "z1", tag=f"rate1_1_{HALF}")
+        for half in halves:
+            nc.scalar.copy(z1[:, half, 0:2], low[:, :, half].rearrange("p s m -> p m s"))
         place(LAST)
 
         def invert(part, diff):
@@ -388,7 +436,7 @@ def tile_list_vacancy_hop_barriers_kernel(
             nc.scalar.activation(part, part, ACT.Abs_reciprocal_sqrt)
 
         quarters = ending[:].rearrange("p (q m) -> p q m", m=QUARTER)
-        home = (10, 11, 9, 4)
+        home = (8, 9, 10, 4)
 
         def slot3(lo, hi):
             return quarters[:, home[lo // QUARTER], lo % QUARTER : lo % QUARTER + hi - lo]
@@ -399,7 +447,7 @@ def tile_list_vacancy_hop_barriers_kernel(
             invert(slot3(lo, hi), slot3(lo, hi))
 
         def product(lo, hi):
-            nc.vector.tensor_tensor(slot3(lo, hi), slot3(lo, hi), rate1[PACK - 1][:, lo:hi], ALU.mult)
+            nc.vector.tensor_tensor(slot3(lo, hi), slot3(lo, hi), rate_last[:, lo:hi], ALU.mult)
 
         def weave(lo, hi):
             q = lo // QUARTER
@@ -409,20 +457,15 @@ def tile_list_vacancy_hop_barriers_kernel(
         def pack(lo, hi):
             quantise_z(1, z1[:, lo:hi, :], lo, hi, sb([P, hi - lo], U32, f"codes1_{lo}")[:])
 
-        def first_pass(q, tag):
-            lo, hi = HALF * q, HALF * (q + 1)
-            quantise_z(0, z0[:, lo:hi, :], lo, hi, sb([P, HALF], U32, "codes0", tag=tag)[:])
-            for m0 in range(lo, hi, P):
-                add_pass(0, m0)
-
-        fetch_origins(LAST, row(feats_tag(PACK), QUARTER), 0, QUARTER)
-        fetch_origins(LAST, row(feats_tag(PACK + 1), QUARTER), QUARTER, HALF)
+        first_pass(1, f"rate1_2_{HALF}")
+        early = row(f"rate1_2_{HALF + QUARTER}", HALF)
+        fetch_origins(LAST, early[:, 0:QUARTER], 0, QUARTER)
+        fetch_origins(LAST, row("g1", QUARTER), QUARTER, HALF)
         difference(0, 256)
         difference(256, 512)
-        fetch_origins(LAST, row(feats_tag(PACK), HALF), HALF, HOPS)
-        first_pass(0, feats_tag(PACK + 1))
-        difference(512, 768)
+        fetch_origins(LAST, early[:, 0:HALF], HALF, HOPS)
         product(0, 256)
+        difference(512, 768)
         product(256, 512)
         weave(0, 256)
         difference(768, 896)
@@ -431,7 +474,6 @@ def tile_list_vacancy_hop_barriers_kernel(
         weave(256, 512)
         product(512, 768)
         pack(256, 512)
-        first_pass(1, feats_tag(PACK))
         weave(512, 768)
         product(768, 896)
         product(896, 1024)
@@ -440,5 +482,5 @@ def tile_list_vacancy_hop_barriers_kernel(
         weave(896, 1024)
         pack(768, 896)
         pack(896, 1024)
-        for lo, hi in ((0, 128), (128, 256), (256, 512), (512, 768), (768, 896), (896, 1024)):
+        for lo, hi in ((0, 128), (128, 256), (256, 512), (512, 640), (640, 768), (768, 896), (896, 1024)):
             score(lo, hi)

@@ -55,13 +55,13 @@ def tile_list_vacancy_hop_barriers_kernel(
         nc.vector.memset(tab_sc[:].bitcast(I32), 0)
         load_list("ions", offs)
         landed_sc = sb([P, T], U8, "landed_sc")
+        pages = [sb([P, T2], F32, "page0")]
+        nc.vector.memset(pages[0][:], 0.0)
         for q in range(4):
             rows = slice(32 * q, 32 * q + 8)
             nc.sync.dma_start(landed_sc[rows, :].bitcast(I32), tab_scales[:, 4 * q : 4 * q + 4, :].bitcast(I32))
             nc.vector.tensor_copy(tab_sc[rows, :].bitcast(I32), landed_sc[rows, :].bitcast(I32))
-        pages = [sb([P, T2], F32, "page0", tag="landed_sc")]
-        nc.gpsimd.memset(pages[0][:], 0.0)
-        ident = sb([P, P], F32, "ident")
+        ident = sb([P, P], F32, "ident", tag="landed_sc")
         make_identity(nc, ident[:])
 
         tab_w = [sb([P, T], U32, "tab_w0", tag="z0_turned"), sb([P, T], U32, "tab_w1", tag="page1")]
@@ -93,7 +93,7 @@ def tile_list_vacancy_hop_barriers_kernel(
             nc.sync.dma_start(dealt_w[QUAD * q : QUAD * (q + 1), :, :], wgs.rearrange("(q t) j -> q t j", t=PACK))
         rate_rows = rate[KP:H, :].rearrange("(p t) m -> p t m", t=PACK)
         ending = sb([P, 3 * HOPS], F32, "ending")
-        rate_cuts = {0: (0, HALF, HOPS), 1: (0, HALF, HOPS), 2: (0, HALF, HALF + QUARTER, HOPS)}
+        rate_cuts = {0: (0, HALF, HOPS), 1: (0, HALF, HOPS), 2: tuple(range(0, HOPS + 1, QUARTER))}
         rate1 = {}
         for t, cuts in rate_cuts.items():
             for lo, hi in zip(cuts, cuts[1:]):
@@ -105,7 +105,7 @@ def tile_list_vacancy_hop_barriers_kernel(
         w4_w = sb([P, PASSES, 2 * N], U8, "w4_w")
         nc.sync.dma_start(w4_w[:].bitcast(I32), w4_words.rearrange("a p n -> p a n").bitcast(I32))
         w4_sc = sb([P, PASSES, N], U8, "w4_sc")
-        nc.gpsimd.memset(w4_sc[:].rearrange("p a n -> p (a n)").bitcast(I32), 0)
+        nc.vector.memset(w4_sc[:].rearrange("p a n -> p (a n)").bitcast(I32), 0)
         for q in range(4):
             nc.sync.dma_start(
                 w4_sc[32 * q : 32 * q + 4, :, :].bitcast(I32),
@@ -240,18 +240,22 @@ def tile_list_vacancy_hop_barriers_kernel(
         halves = [slice(lo, lo + HALF) for lo in range(0, HOPS, HALF)]
         damps = {}
 
+        def turn_in(k, lo, hi):
+            diff = ring([P, hi - lo], "diff")
+            half = lo - lo % HALF
+            for m in range(lo, hi, P):
+                pair = (targets[k, half][:, m - half : m - half + P], origins[k, 0][:, m : m + P])
+                for i, side in enumerate(pair):
+                    nc.tensor.matmul(
+                        diff[:, m - lo : m - lo + P], side, ident[:], start=i == 0, stop=i == 1, is_transpose=True
+                    )
+            nc.scalar.activation(damps[k][:, lo:hi], diff[:], ACT.Square)
+            nc.scalar.activation(damps[k][:, lo:hi], damps[k][:, lo:hi], ACT.Square, bias=1.0)
+
         def differ(k):
             damps[k] = damp_tile()
             for half in halves:
-                diff = ring([P, HALF], "diff")
-                for m in range(0, HALF, P):
-                    cols = slice(half.start + m, half.start + m + P)
-                    origin = origins[k, half.start][:, m : m + P] if (k, half.start) in origins else origins[k, 0][:, cols]
-                    pair = (targets[k, half.start][:, m : m + P], origin)
-                    for i, side in enumerate(pair):
-                        nc.tensor.matmul(diff[:, m : m + P], side, ident[:], start=i == 0, stop=i == 1, is_transpose=True)
-                nc.scalar.activation(damps[k][:, half], diff[:], ACT.Square)
-                nc.scalar.activation(damps[k][:, half], damps[k][:, half], ACT.Square, bias=1.0)
+                turn_in(k, half.start, half.stop)
 
         def weigh_turned(k):
             damp = damps[k]
@@ -264,18 +268,15 @@ def tile_list_vacancy_hop_barriers_kernel(
                 ALU.mult,
             )
 
-        def weigh_slot(k):
-            damp = damps[k]
-            for half in halves:
-                back = ring([P, HALF], "back")
-                for m in range(0, HALF, P):
-                    nc.tensor.transpose(back[:, m : m + P], damp[:, half.start + m : half.start + m + P], ident[:])
-                part = low[:, k - PACK, half]
-                nc.scalar.activation(part, back[:], ACT.Abs_reciprocal_sqrt)
-                cuts = [c for c in rate_cuts[k - PACK] if half.start <= c <= half.stop]
-                for lo, hi in zip(cuts, cuts[1:]):
-                    piece = low[:, k - PACK, lo:hi]
-                    nc.gpsimd.tensor_tensor(piece, piece, rate1[k - PACK, lo][:], ALU.mult)
+        def turn_out(k, lo, hi, values, result):
+            if k == LAST - 1:
+                back = psum.tile([P, hi - lo], F32, name="back", tag="acc", bufs=6)
+            else:
+                back = ring([P, hi - lo], "back")
+            for m in range(lo, hi, P):
+                nc.tensor.transpose(back[:, m - lo : m - lo + P], damps[k][:, m : m + P], ident[:])
+            nc.scalar.activation(values[:, lo:hi], back[:], ACT.Abs_reciprocal_sqrt)
+            nc.gpsimd.tensor_tensor(result[:, lo:hi], values[:, lo:hi], rate1[k - PACK, lo][:], ALU.mult)
 
         z_mx = {}
 
@@ -326,8 +327,8 @@ def tile_list_vacancy_hop_barriers_kernel(
                 nc.scalar.copy(rate0[k][:, lo : lo + HALF], turn[:])
 
 
-        def turn_back():
-            for j0 in range(0, HOPS // P, 2):
+        def turn_back(i):
+            for j0 in range(PACK * i, PACK * (i + 1), 2):
                 bank = ring([P, 2, 2, P], "words")
                 for j in range(2):
                     words = z0_turned[:, j0 + j, :].bitcast(F32)
@@ -373,9 +374,6 @@ def tile_list_vacancy_hop_barriers_kernel(
         fetch_origins(1, row(origin_tags[1]))
         fetch_targets(1, row("g2_sc"))
         fetch_origins(2, row(origin_tags[0]))
-        preweigh(3, feats_tag(2))
-        preweigh(4, feats_tag(1))
-        preweigh(5, "raw128_1")
         z0_turned = sb([P, HOPS // P, KP], BF16, "z0_turned")
         weigh_turned(0)
         z0 = [sb([P, HALF, PACK], BF16, "z0", tag=tag) for tag in ("got_w0", "g1")]
@@ -384,48 +382,35 @@ def tile_list_vacancy_hop_barriers_kernel(
                 turn_rate(k)
             differ(k)
             weigh_turned(k)
-            if k > 1:
-                preweigh(k + PACK, f"rate0_{k}")
-            place(k + 2)
-            target = row("g2_sc")
-            fetch_targets(k + 1, target[:, 0:HALF], 0, HALF)
             if k == PACK - 1:
-                fetch_origins(k + 2, row(origin_tags[k % 2], 2 * HOPS)[:, 0:HOPS])
-            fetch_targets(k + 1, target[:, HALF:HOPS], HALF, HOPS)
+                preweigh(LAST, f"rate0_{k}")
+            place(k + 2)
+            fetch_targets(k + 1, row("g2_sc"))
             if k < PACK - 1:
                 fetch_origins(k + 2, row(origin_tags[k % 2]))
-
-        def invert_halves(diff, result):
-            for half in halves:
-                nc.scalar.activation(diff[:, half], diff[:, half], ACT.Square)
-            for half in halves:
-                nc.scalar.activation(diff[:, half], diff[:, half], ACT.Square, bias=1.0)
-            for half in halves:
-                nc.scalar.activation(result[:, half], diff[:, half], ACT.Abs_reciprocal_sqrt)
-
-        def times_rate(k, result, values):
-            cuts = rate_cuts[k - PACK]
-            for lo, hi in zip(cuts, cuts[1:]):
-                nc.gpsimd.tensor_tensor(result[:, lo:hi], values[:, lo:hi], rate1[k - PACK, lo][:], ALU.mult)
-
-        diff5 = row("g2")
-        fetch_difference(5, origins[5, 0], diff5, 0, HOPS)
+        both = row(origin_tags[1], 2 * HOPS)
+        fetch_origins(5, both[:, 0:HOPS])
+        fetch_targets(5, both[:, HOPS : 2 * HOPS])
         place(6)
+        fetch_origins(6, row(feats_tag(PACK - 1)))
+        low = sb([P, 2, HOPS], F32, "low", tag="g2")
+        differ(4)
+        turn_back(0)
+        fetch_targets(6, row("g2_sc"))
+        differ(5)
         for half in halves:
-            fetch_origins(6, row(feats_tag(PACK - 1 + half.start // HALF), HALF), half.start, half.stop)
-        differ(PACK)
-        low = sb([P, 2, HOPS], F32, "low", tag=origin_tags[1])
-        weigh_slot(PACK)
-        invert_halves(diff5, diff5)
-        times_rate(5, low[:, 1, :], diff5)
-        turn_back()
-        diff6 = row(f"rate1_1_{HALF}")
+            turn_out(4, half.start, half.stop, low[:, 0, :], low[:, 0, :])
+        turn_back(1)
         for half in halves:
-            fetch_difference(6, origins[6, half.start], diff6[:, half], half.start, half.stop)
-        first_pass(0, "g2")
-        invert_halves(diff6, ending)
-        times_rate(6, ending, ending)
-        z1 = sb([P, HOPS, PACK], BF16, "z1", tag=f"rate1_1_{HALF}")
+            turn_out(5, half.start, half.stop, low[:, 1, :], low[:, 1, :])
+        damps[6] = damp_tile()
+        for lo in range(0, HOPS + QUARTER, QUARTER):
+            if lo < HOPS:
+                turn_in(6, lo, lo + QUARTER)
+            if 0 < lo < HOPS:
+                turn_out(6, lo - QUARTER, lo, ending, ending)
+        turn_out(6, HOPS - QUARTER, HOPS, row("roots"), ending)
+        z1 = sb([P, HOPS, PACK], BF16, "z1", tag=f"rate1_2_{HALF}")
         for half in halves:
             nc.scalar.copy(z1[:, half, 0:2], low[:, :, half].rearrange("p s m -> p m s"))
         place(LAST)
@@ -457,15 +442,16 @@ def tile_list_vacancy_hop_barriers_kernel(
         def pack(lo, hi):
             quantise_z(1, z1[:, lo:hi, :], lo, hi, sb([P, hi - lo], U32, f"codes1_{lo}")[:])
 
-        first_pass(1, f"rate1_2_{HALF}")
-        early = row(f"rate1_2_{HALF + QUARTER}", HALF)
+        first_pass(0, f"rate1_2_{HALF + QUARTER}")
+        early = row("roots", HALF)
         fetch_origins(LAST, early[:, 0:QUARTER], 0, QUARTER)
-        fetch_origins(LAST, row("g1", QUARTER), QUARTER, HALF)
+        fetch_origins(LAST, row("got_w0", QUARTER), QUARTER, HALF)
         difference(0, 256)
         difference(256, 512)
         fetch_origins(LAST, early[:, 0:HALF], HALF, HOPS)
-        product(0, 256)
+        first_pass(1, "got_w0")
         difference(512, 768)
+        product(0, 256)
         product(256, 512)
         weave(0, 256)
         difference(768, 896)

@@ -190,7 +190,7 @@ def tile_list_vacancy_hop_barriers_kernel(
             return site_w[:] if k < PACK else dealt_w[:, k - PACK, :]
 
         def page_of(k):
-            return pages[min(k, LAST - 1) % PAGES]
+            return pages[k % PAGES]
 
         weighted = {}
 
@@ -234,8 +234,8 @@ def tile_list_vacancy_hop_barriers_kernel(
         def fetch_difference(k, origin, part, lo, hi):
             nc.vector.tensor_tensor(part, page_of(k)[:].indirect(entries("targets", lo, hi)), origin, ALU.subtract)
 
-        def damp_tile():
-            return sb([P, HOPS], F32, "damp", bufs=2)
+        def damp_tile(k):
+            return sb([P, HOPS], F32, "damp", tag=f"damp{(k if k < PACK else k + 1) % 2}")
 
         halves = [slice(lo, lo + HALF) for lo in range(0, HOPS, HALF)]
         damps = {}
@@ -244,7 +244,8 @@ def tile_list_vacancy_hop_barriers_kernel(
             diff = ring([P, hi - lo], "diff")
             half = lo - lo % HALF
             for m in range(lo, hi, P):
-                pair = (targets[k, half][:, m - half : m - half + P], origins[k, 0][:, m : m + P])
+                first = max(s for kk, s in origins if kk == k and s <= m)
+                pair = (targets[k, half][:, m - half : m - half + P], origins[k, first][:, m - first : m - first + P])
                 for i, side in enumerate(pair):
                     nc.tensor.matmul(
                         diff[:, m - lo : m - lo + P], side, ident[:], start=i == 0, stop=i == 1, is_transpose=True
@@ -253,7 +254,7 @@ def tile_list_vacancy_hop_barriers_kernel(
             nc.scalar.activation(damps[k][:, lo:hi], damps[k][:, lo:hi], ACT.Square, bias=1.0)
 
         def differ(k):
-            damps[k] = damp_tile()
+            damps[k] = damp_tile(k)
             for half in halves:
                 turn_in(k, half.start, half.stop)
 
@@ -392,18 +393,20 @@ def tile_list_vacancy_hop_barriers_kernel(
         fetch_origins(5, both[:, 0:HOPS])
         fetch_targets(5, both[:, HOPS : 2 * HOPS])
         place(6)
-        fetch_origins(6, row(feats_tag(PACK - 1)))
+        fetch_targets(6, row("g2_sc"))
+        whole = row(feats_tag(PACK - 1))
+        for lo, hi in ((0, HALF), (HALF, HALF + QUARTER), (HALF + QUARTER, HOPS)):
+            fetch_origins(6, whole[:, lo:hi], lo, hi)
         low = sb([P, 2, HOPS], F32, "low", tag="g2")
         differ(4)
         turn_back(0)
-        fetch_targets(6, row("g2_sc"))
         differ(5)
         for half in halves:
             turn_out(4, half.start, half.stop, low[:, 0, :], low[:, 0, :])
         turn_back(1)
         for half in halves:
             turn_out(5, half.start, half.stop, low[:, 1, :], low[:, 1, :])
-        damps[6] = damp_tile()
+        damps[6] = damp_tile(6)
         for lo in range(0, HOPS + QUARTER, QUARTER):
             if lo < HOPS:
                 turn_in(6, lo, lo + QUARTER)

@@ -93,12 +93,12 @@ def tile_list_vacancy_hop_barriers_kernel(
             nc.sync.dma_start(dealt_w[QUAD * q : QUAD * (q + 1), :, :], wgs.rearrange("(q t) j -> q t j", t=PACK))
         rate_rows = rate[KP:H, :].rearrange("(p t) m -> p t m", t=PACK)
         ending = sb([P, 3 * HOPS], F32, "ending")
-        rate_cuts = {0: (0, HALF, HOPS), 1: (0, HALF, HOPS), 2: tuple(range(0, HOPS + 1, QUARTER))}
+        rate_low = sb([P, 2, HOPS], F32, "rate_low")
+        nc.sync.dma_start(rate_low[:], rate_rows[:, 0:2, :])
         rate1 = {}
-        for t, cuts in rate_cuts.items():
-            for lo, hi in zip(cuts, cuts[1:]):
-                rate1[t, lo] = sb([P, hi - lo], F32, f"rate1_{t}_{lo}")
-                nc.sync.dma_start(rate1[t, lo][:], rate_rows[:, t, lo:hi])
+        for lo in range(0, HOPS, QUARTER):
+            rate1[2, lo] = sb([P, QUARTER], F32, f"rate1_2_{lo}")
+            nc.sync.dma_start(rate1[2, lo][:], rate_rows[:, 2, lo : lo + QUARTER])
         rate_last = ending[:, HOPS : 2 * HOPS]
         nc.sync.dma_start(rate_last, rate_rows[:, PACK - 1, :])
 
@@ -277,7 +277,8 @@ def tile_list_vacancy_hop_barriers_kernel(
             for m in range(lo, hi, P):
                 nc.tensor.transpose(back[:, m - lo : m - lo + P], damps[k][:, m : m + P], ident[:])
             nc.scalar.activation(values[:, lo:hi], back[:], ACT.Abs_reciprocal_sqrt)
-            nc.gpsimd.tensor_tensor(result[:, lo:hi], values[:, lo:hi], rate1[k - PACK, lo][:], ALU.mult)
+            if k == LAST - 1:
+                nc.gpsimd.tensor_tensor(result[:, lo:hi], values[:, lo:hi], rate1[k - PACK, lo][:], ALU.mult)
 
         z_mx = {}
 
@@ -393,19 +394,27 @@ def tile_list_vacancy_hop_barriers_kernel(
         fetch_origins(5, both[:, 0:HOPS])
         fetch_targets(5, both[:, HOPS : 2 * HOPS])
         place(6)
-        fetch_targets(6, row("g2_sc"))
-        whole = row(feats_tag(PACK - 1))
-        for lo, hi in ((0, HALF), (HALF, HALF + QUARTER), (HALF + QUARTER, HOPS)):
-            fetch_origins(6, whole[:, lo:hi], lo, hi)
+        far, whole = row("g2_sc"), row(feats_tag(PACK - 1))
+        fetch_targets(6, far[:, 0:HALF], 0, HALF)
+        fetch_origins(6, whole[:, 0:HALF], 0, HALF)
+        fetch_targets(6, far[:, HALF:HOPS], HALF, HOPS)
+        for lo in range(HALF, HOPS, QUARTER):
+            fetch_origins(6, whole[:, lo : lo + QUARTER], lo, lo + QUARTER)
         low = sb([P, 2, HOPS], F32, "low", tag="g2")
         differ(4)
         turn_back(0)
         differ(5)
-        for half in halves:
-            turn_out(4, half.start, half.stop, low[:, 0, :], low[:, 0, :])
+        z1 = sb([P, HOPS, PACK], BF16, "z1", tag="raw512_0")
+        for h, half in enumerate(halves):
+            for k in (4, 5):
+                turn_out(k, half.start, half.stop, low[:, k - PACK, :], low[:, k - PACK, :])
+            nc.gpsimd.tensor_tensor(
+                z1[:, half, 0:2].rearrange("p (c i) s -> p c s i", i=PACK),
+                low[:, :, half].rearrange("p s (c i) -> p c s i", i=PACK),
+                rate_low[:, :, half].rearrange("p s (c i) -> p c s i", i=PACK),
+                ALU.mult,
+            )
         turn_back(1)
-        for half in halves:
-            turn_out(5, half.start, half.stop, low[:, 1, :], low[:, 1, :])
         damps[6] = damp_tile(6)
         for lo in range(0, HOPS + QUARTER, QUARTER):
             if lo < HOPS:
@@ -413,9 +422,6 @@ def tile_list_vacancy_hop_barriers_kernel(
             if 0 < lo < HOPS:
                 turn_out(6, lo - QUARTER, lo, ending, ending)
         turn_out(6, HOPS - QUARTER, HOPS, row("roots"), ending)
-        z1 = sb([P, HOPS, PACK], BF16, "z1", tag=f"rate1_2_{HALF}")
-        for half in halves:
-            nc.scalar.copy(z1[:, half, 0:2], low[:, :, half].rearrange("p s m -> p m s"))
         place(LAST)
 
         def invert(part, diff):

@@ -53,7 +53,6 @@ def tile_list_vacancy_hop_barriers_kernel(
 
         tab_sc = sb([P, T], U8, "tab_sc")
         nc.vector.memset(tab_sc[:].bitcast(I32), 0)
-        load_list("ions", offs)
         landed_sc = sb([P, T], U8, "landed_sc")
         pages = [sb([P, T2], F32, "page0")]
         nc.vector.memset(pages[0][:], 0.0)
@@ -74,15 +73,16 @@ def tile_list_vacancy_hop_barriers_kernel(
             nc.sync.dma_start(raw[:], w1[KP * a : KP * (a + 1), lo:hi].rearrange("(p j) c -> p j c", j=PACK))
             return raw
 
+        for name, src in (("ions", offs), ("sites", offs2), ("origins", offs3)):
+            load_list(name, src)
+        raw_head = [load_w1(0, 0, P)]
         load_tab(0)
-        raw_head = [load_w1(a, 0, P) for a in range(PASSES)]
+        raw_head.append(load_w1(1, 0, P))
         load_tab(1)
-        load_list("sites", offs2)
         site_w = sb([P, S], F32, "site_w")
         for lo in range(0, S, HALF):
             nc.sync.dma_start(site_w[:, lo : lo + HALF], wgs[:, lo : lo + HALF])
         raw_mid = [load_w1(a, P, HALF) for a in range(PASSES)]
-        load_list("origins", offs3)
         load_list("targets", offs4)
         raw_end = [load_w1(a, HALF, H) for a in range(PASSES)]
         rate0 = [sb([P, HOPS], F32, f"rate0_{k}") for k in range(PACK)]

@@ -58,7 +58,14 @@ def tile_list_vacancy_hop_barriers_kernel(
         nc.vector.memset(pages[0][:], 0.0)
         for q in range(4):
             rows = slice(32 * q, 32 * q + 8)
-            nc.sync.dma_start(landed_sc[rows, :].bitcast(I32), tab_scales[:, 4 * q : 4 * q + 4, :].bitcast(I32))
+            if q < 2:
+                nc.sync.dma_start(landed_sc[rows, :].bitcast(I32), tab_scales[:, 4 * q : 4 * q + 4, :].bitcast(I32))
+            else:
+                for a in range(PASSES):
+                    nc.sync.dma_start(
+                        landed_sc[32 * q + 4 * a : 32 * q + 4 * a + 4, :].bitcast(I32),
+                        tab_scales[a, 4 * q : 4 * q + 4, :].bitcast(I32),
+                    )
             nc.vector.tensor_copy(tab_sc[rows, :].bitcast(I32), landed_sc[rows, :].bitcast(I32))
         ident = sb([P, P], F32, "ident", tag="landed_sc")
         make_identity(nc, ident[:])
@@ -73,16 +80,17 @@ def tile_list_vacancy_hop_barriers_kernel(
             nc.sync.dma_start(raw[:], w1[KP * a : KP * (a + 1), lo:hi].rearrange("(p j) c -> p j c", j=PACK))
             return raw
 
-        for name, src in (("ions", offs), ("sites", offs2), ("origins", offs3)):
-            load_list(name, src)
+        load_list("ions", offs)
         raw_head = [load_w1(0, 0, P)]
         load_tab(0)
         raw_head.append(load_w1(1, 0, P))
         load_tab(1)
+        load_list("sites", offs2)
         site_w = sb([P, S], F32, "site_w")
         for lo in range(0, S, HALF):
             nc.sync.dma_start(site_w[:, lo : lo + HALF], wgs[:, lo : lo + HALF])
         raw_mid = [load_w1(a, P, HALF) for a in range(PASSES)]
+        load_list("origins", offs3)
         load_list("targets", offs4)
         raw_end = [load_w1(a, HALF, H) for a in range(PASSES)]
         rate0 = [sb([P, HOPS], F32, f"rate0_{k}") for k in range(PACK)]

from contextlib import ExitStack

import concourse.mybir as mybir
from concourse.masks import make_identity

K, H, N, T, S, T2, HOPS = 1024, 1024, 384, 2048, 1024, 2048, 1024
FLOPS = 2 * K * H * S + 2 * H * N * HOPS

F32 = mybir.dt.float32
BF16 = mybir.dt.bfloat16
I32 = mybir.dt.int32
U32 = mybir.dt.uint32
U16 = mybir.dt.uint16
U8 = mybir.dt.uint8
FP8X4 = mybir.dt.float8_e4m3fn_x4
FP4X4 = mybir.dt.float4_e2m1fn_x4
ACT = mybir.ActivationFunctionType
ALU = mybir.AluOpType

P = 128
PACK = 4
KP = P * PACK
PASSES = 2
HALF = 512
NT = N // P
QUAD = P // PACK
BLOCKS = H // P
LAST = BLOCKS - 1
PAGES = 2
HEAD_CUTS = ((0, 256), (256, 512), (512, 1024))
QUARTER = 256


def tile_list_vacancy_hop_barriers_kernel(
    tc, tab_words, tab_scales, offs, offs2, offs3, offs4, w1, wgs, rate, w4_words, w4_scales, out
):
    nc = tc.nc
    with ExitStack() as ctx:
        keep = ctx.enter_context(tc.tile_pool(name="keep", bufs=1))
        psum = ctx.enter_context(tc.psum_pool(name="psum", bufs=2))

        def sb(shape, dtype, name, tag=None, bufs=1):
            return keep.tile(shape, dtype, name=name, tag=tag or name, bufs=bufs, align_bytes=64)

        lists = {}

        def load_list(name, src):
            lists[name] = keep.tile([P, S // 16], U16, name=name)
            nc.sync.dma_start(lists[name][:], src)

        def entries(name, lo, hi):
            return lists[name][:, lo // 16 : hi // 16]

        tab_sc = sb([P, T], U8, "tab_sc")
        nc.vector.memset(tab_sc[:].bitcast(I32), 0)
        landed_sc = sb([P, T], U8, "landed_sc")
        pages = [sb([P, T2], F32, "page0")]
        nc.vector.memset(pages[0][:], 0.0)
        for q in range(4):
            rows = slice(32 * q, 32 * q + 8)
            if q < 2:
                nc.sync.dma_start(landed_sc[rows, :].bitcast(I32), tab_scales[:, 4 * q : 4 * q + 4, :].bitcast(I32))
            else:
                for a in range(PASSES):
                    nc.sync.dma_start(
                        landed_sc[32 * q + 4 * a : 32 * q + 4 * a + 4, :].bitcast(I32),
                        tab_scales[a, 4 * q : 4 * q + 4, :].bitcast(I32),
                    )
            nc.vector.tensor_copy(tab_sc[rows, :].bitcast(I32), landed_sc[rows, :].bitcast(I32))
        ident = sb([P, P], F32, "ident", tag="landed_sc")
        make_identity(nc, ident[:])

        tab_w = [sb([P, T], U32, "tab_w0", tag="z0_turned"), sb([P, T], U32, "tab_w1", tag="page1")]

        def load_tab(a):
            nc.sync.dma_start(tab_w[a][:].bitcast(I32), tab_words[a].rearrange("p t i -> p (t i)").bitcast(I32))

        def load_w1(a, lo, hi):
            raw = sb([P, PACK, hi - lo], F32, f"raw{lo}_{a}")
            nc.sync.dma_start(raw[:], w1[KP * a : KP * (a + 1), lo:hi].rearrange("(p j) c -> p j c", j=PACK))
            return raw

        load_list("ions", offs)
        raw_head = [load_w1(0, 0, P)]
        load_tab(0)
        raw_head.append(load_w1(1, 0, P))
        load_tab(1)
        load_list("sites", offs2)
        site_w = sb([P, S], F32, "site_w")
        for lo in range(0, S, HALF):
            nc.sync.dma_start(site_w[:, lo : lo + HALF], wgs[:, lo : lo + HALF])
        raw_mid = [load_w1(a, P, HALF) for a in range(PASSES)]
        load_list("origins", offs3)
        load_list("targets", offs4)
        raw_end = [load_w1(a, HALF, H) for a in range(PASSES)]
        rate0 = [sb([P, HOPS], F32, f"rate0_{k}") for k in range(PACK)]
        for k in range(PACK):
            nc.sync.dma_start(rate0[k][:], rate[P * k : P * (k + 1), :])
        dealt_w = sb([P, PACK, S], F32, "dealt_w")
        for q in range(PACK):
            nc.sync.dma_start(dealt_w[QUAD * q : QUAD * (q + 1), :, :], wgs.rearrange("(q t) j -> q t j", t=PACK))
        rate_rows = rate[KP:H, :].rearrange("(p t) m -> p t m", t=PACK)
        ending = sb([P, 3 * HOPS], F32, "ending")
        rate_low = sb([P, 2, HOPS], F32, "rate_low")
        nc.sync.dma_start(rate_low[:], rate_rows[:, 0:2, :])
        rate1 = {}
        for lo in range(0, HOPS, QUARTER):
            rate1[2, lo] = sb([P, QUARTER], F32, f"rate1_2_{lo}")
            nc.sync.dma_start(rate1[2, lo][:], rate_rows[:, 2, lo : lo + QUARTER])
        rate_last = ending[:, HOPS : 2 * HOPS]
        nc.sync.dma_start(rate_last, rate_rows[:, PACK - 1, :])

        w4_w = sb([P, PASSES, 2 * N], U8, "w4_w")
        nc.sync.dma_start(w4_w[:].bitcast(I32), w4_words.rearrange("a p n -> p a n").bitcast(I32))
        w4_sc = sb([P, PASSES, N], U8, "w4_sc")
        nc.vector.memset(w4_sc[:].rearrange("p a n -> p (a n)").bitcast(I32), 0)
        for q in range(4):
            nc.sync.dma_start(
                w4_sc[32 * q : 32 * q + 4, :, :].bitcast(I32),
                w4_scales[:, 4 * q : 4 * q + 4, :].rearrange("a r n -> r a n").bitcast(I32),
            )

        got_sc = sb([P, S], U8, "got_sc")
        nc.vector.tensor_copy(got_sc[:], tab_sc[:].indirect(entries("ions", 0, S)))
        got_w0 = sb([P, S], U32, "got_w0")
        nc.vector.tensor_copy(got_w0[:], tab_w[0][:].indirect(entries("ions", 0, S)))

        w1_mx = {}

        grouped = {}

        def round_w1(name, raw, first, blocks, c0, i, count, tag=None):
            width = P * blocks
            if name not in grouped:
                grouped[name] = sb([P, count, width, PACK], BF16, name, tag=tag)
            src = raw[:, :, c0 : c0 + width]
            if first >= PACK:
                nc.scalar.copy(
                    grouped[name][:, i].rearrange("p (t m) j -> p m t j", t=PACK),
                    src.rearrange("p j (m t) -> p m t j", t=PACK),
                )
            else:
                nc.scalar.copy(
                    grouped[name][:, i].rearrange("p (c i) j -> p c j i", i=PACK),
                    src.rearrange("p j (c i) -> p c j i", i=PACK),
                )

        def pack_w1(name, first, blocks, passes):
            width = P * blocks
            codes = sb([P, len(passes) * width], U32, name + "_codes")
            scales = sb([P, len(passes) * width], U8, name + "_sc")
            nc.vector.quantize_mx(
                out=codes[:].bitcast(FP8X4), scales=scales[:], in_=grouped[name][:].rearrange("p a c j -> p (a c j)")
            )
            for i, a in enumerate(passes):
                for b in range(blocks):
                    cols = slice(width * i + P * b, width * i + P * (b + 1))
                    w1_mx[first + b, a] = (codes[:, cols], scales[:, cols])

        for a in range(PASSES):
            round_w1("g0", raw_head[a], 0, 1, 0, a, PASSES)
        pack_w1("g0", 0, 1, (0, 1))

        got_w1 = sb([P, S], U32, "got_w1")
        for lo, hi in HEAD_CUTS:
            nc.vector.tensor_copy(got_w1[:, lo:hi], tab_w[1][:].indirect(entries("ions", lo, hi)))

        pages.append(sb([P, T2], F32, "page1"))
        nc.gpsimd.memset(pages[1][:], 0.0)

        feats = {}

        def feats_tag(k):
            return f"raw512_{k - 1}" if k in (1, 2) else f"feats{k}"

        def ring(shape, name):
            return psum.tile(shape, F32, name=name, tag="ring", bufs=2)

        def features(k):
            feats[k] = sb([P, S], F32, f"feats{k}", tag=feats_tag(k))
            for lo, hi in HEAD_CUTS if k == 0 else ((0, HALF), (HALF, S)):
                cols = slice(lo, hi)
                acc = ring([P, hi - lo], "acc1")
                for a in range(PASSES):
                    codes, scales = w1_mx[k, a]
                    nc.tensor.matmul_mx(
                        out=acc[:],
                        lhsT=codes.bitcast(FP8X4),
                        lhsT_scale=scales,
                        rhs=(got_w0, got_w1)[a][:, cols].bitcast(FP8X4),
                        rhs_scale=got_sc[4 * a : P, cols],
                        start=(a == 0),
                        stop=(a == PASSES - 1),
                    )
                nc.scalar.activation(feats[k][:, cols], acc[:], ACT.Silu)

        def weights(k):
            return site_w[:] if k < PACK else dealt_w[:, k - PACK, :]

        def page_of(k):
            return pages[k % PAGES]

        weighted = {}

        def preweigh(k, tag):
            weighted[k] = sb([P, S], F32, "weighted", tag=tag)
            nc.gpsimd.tensor_tensor(weighted[k][:], feats[k][:], weights(k), ALU.mult)

        def place(k):
            page = page_of(k)
            if k in weighted:
                nc.vector.tensor_copy(page[:].indirect(entries("sites", 0, S)), weighted[k][:])
                return
            first = HEAD_CUTS[0][1]
            for lo, hi in ((0, first), (first, S)) if k == 0 else ((0, S),):
                nc.vector.tensor_tensor(
                    page[:].indirect(entries("sites", lo, hi)), feats[k][:, lo:hi], weights(k)[:, lo:hi], ALU.mult
                )

        origins = {}
        targets = {}

        def row(tag, width=HOPS):
            return sb([P, width], F32, "row", tag=tag)[:]

        def fetch_origins(k, into, lo=0, hi=HOPS):
            origins[k, lo] = into
            nc.vector.tensor_copy(into, page_of(k)[:].indirect(entries("origins", lo, hi)))

        def fetch_targets(k, both, first=0, end=HOPS):
            for lo in range(first, end, HALF):
                targets[k, lo] = both[:, lo - first : lo - first + HALF]
                nc.vector.tensor_scalar(
                    targets[k, lo],
                    page_of(k)[:].indirect(entries("targets", lo, lo + HALF)),
                    -1.0,
                    0.0,
                    ALU.mult,
                    ALU.add,
                )

        def fetch_difference(k, origin, part, lo, hi):
            nc.vector.tensor_tensor(part, page_of(k)[:].indirect(entries("targets", lo, hi)), origin, ALU.subtract)

        def damp_tile(k):
            return sb([P, HOPS], F32, "damp", tag=f"damp{(k if k < PACK else k + 1) % 2}")

        halves = [slice(lo, lo + HALF) for lo in range(0, HOPS, HALF)]
        damps = {}

        def turn_in(k, lo, hi):
            diff = ring([P, hi - lo], "diff")
            half = lo - lo % HALF
            for m in range(lo, hi, P):
                first = max(s for kk, s in origins if kk == k and s <= m)
                pair = (targets[k, half][:, m - half : m - half + P], origins[k, first][:, m - first : m - first + P])
                for i, side in enumerate(pair):
                    nc.tensor.matmul(
                        diff[:, m - lo : m - lo + P], side, ident[:], start=i == 0, stop=i == 1, is_transpose=True
                    )
            nc.scalar.activation(damps[k][:, lo:hi], diff[:], ACT.Square)
            nc.scalar.activation(damps[k][:, lo:hi], damps[k][:, lo:hi], ACT.Square, bias=1.0)

        def differ(k):
            damps[k] = damp_tile(k)
            for half in halves:
                turn_in(k, half.start, half.stop)

        def weigh_turned(k):
            damp = damps[k]
            for half in halves:
                nc.scalar.activation(damp[:, half], damp[:, half], ACT.Abs_reciprocal_sqrt)
            nc.gpsimd.tensor_tensor(
                z0_turned[:, :, P * k : P * (k + 1)],
                damp[:].rearrange("m (j r) -> m j r", r=P),
                rate0[k][:].rearrange("m (j r) -> m j r", r=P),
                ALU.mult,
            )

        def turn_out(k, lo, hi, values, result):
            if k == LAST - 1:
                back = psum.tile([P, hi - lo], F32, name="back", tag="acc", bufs=6)
            else:
                back = ring([P, hi - lo], "back")
            for m in range(lo, hi, P):
                nc.tensor.transpose(back[:, m - lo : m - lo + P], damps[k][:, m : m + P], ident[:])
            nc.scalar.activation(values[:, lo:hi], back[:], ACT.Abs_reciprocal_sqrt)
            if k == LAST - 1:
                nc.gpsimd.tensor_tensor(result[:, lo:hi], values[:, lo:hi], rate1[k - PACK, lo][:], ALU.mult)

        z_mx = {}

        def quantise_z(b, z, lo, hi, codes):
            scales = sb([P, hi - lo], U8, f"z_sc{b}_{lo}")
            nc.vector.quantize_mx(
                out=codes.bitcast(FP8X4), scales=scales[:], in_=z.rearrange("p m t -> p (m t)")
            )
            for m in range(lo, hi, P):
                z_mx[b, m] = (codes[:, m - lo : m - lo + P], scales[:, m - lo : m - lo + P])

        sums = {}

        def add_pass(a, m0):
            if a == 0:
                if m0 < 6 * P:
                    sums[m0] = psum.tile([P, NT, P], F32, name="acc2", tag="acc", bufs=6)
                else:
                    sums[m0] = ring([P, NT, P], "acc2")
            codes, scales = z_mx[a, m0]
            for n in range(NT):
                nc.tensor.matmul_mx(
                    out=sums[m0][:, n, :],
                    lhsT=w4_w[:, a, 2 * P * n : 2 * P * (n + 1)].bitcast(FP4X4),
                    lhsT_scale=w4_sc[:, a, P * n : P * (n + 1)],
                    rhs=codes.bitcast(FP8X4),
                    rhs_scale=scales,
                    start=(a == 0 and n == 0),
                    stop=(a == PASSES - 1 and n == NT - 1),
                )

        def score(lo, hi):
            staged = sb([P, NT, hi - lo], F32, f"staged{lo}")
            for m0 in range(lo, hi, P):
                add_pass(1, m0)
                part = staged[:, :, m0 - lo : m0 - lo + P]
                if m0 + P == HOPS:
                    nc.vector.tensor_copy(part, sums[m0][:])
                else:
                    nc.scalar.copy(part, sums[m0][:])
            nc.sync.dma_start(out.rearrange("(n p) m -> p n m", p=P)[:, :, lo:hi], staged[:])

        def turn_rate(k):
            for lo in range(0, HOPS, HALF):
                turn = ring([P, HALF], "rate_turn")
                for m in range(0, HALF, P):
                    nc.tensor.transpose(turn[:, m : m + P], rate0[k][:, lo + m : lo + m + P], ident[:])
                nc.scalar.copy(rate0[k][:, lo : lo + HALF], turn[:])


        def turn_back(i):
            for j0 in range(PACK * i, PACK * (i + 1), 2):
                bank = ring([P, 2, 2, P], "words")
                for j in range(2):
                    words = z0_turned[:, j0 + j, :].bitcast(F32)
                    for u in range(2):
                        nc.tensor.transpose(bank[:, j, u, :], words[:, u : KP // 2 : 2], ident[:])
                nc.scalar.copy(
                    z0[j0 // PACK][:, P * (j0 % PACK) : P * (j0 % PACK + 2), :].bitcast(F32).rearrange("p (j m) u -> p j m u", m=P),
                    bank[:].rearrange("p j u m -> p j m u"),
                )

        def first_pass(q, tag):
            lo, hi = HALF * q, HALF * (q + 1)
            quantise_z(0, z0[q][:], lo, hi, sb([P, HALF], U32, "codes0", tag=tag)[:])
            for m0 in range(lo, hi, P):
                add_pass(0, m0)

        features(0)
        place(0)
        round_w1("g1", raw_mid[0], 1, 1, 0, 0, PASSES)
        for a in range(PASSES):
            round_w1("g2", raw_mid[a], 2, 2, P, a, PASSES)
        round_w1("g1", raw_mid[1], 1, 1, 0, 1, PASSES)
        pack_w1("g2", 2, 2, (0, 1))
        pack_w1("g1", 1, 1, (0, 1))
        both = row("g2", 2 * HOPS)
        fetch_origins(0, both[:, 0:HOPS])
        fetch_targets(0, both[:, HOPS : 2 * HOPS])
        round_w1("g4", raw_end[0], PACK, PACK, 0, 0, 1)
        pack_w1("g4", PACK, PACK, (0,))
        features(1)
        place(1)
        round_w1("g5", raw_end[1], PACK, PACK, 0, 0, 1, tag="g4")
        pack_w1("g5", PACK, PACK, (1,))
        features(2)
        features(3)
        turn_rate(0)
        turn_rate(1)
        for k in range(PACK, BLOCKS):
            features(k)
        differ(0)
        origin_tags = ("g4", "g2_codes")
        place(2)
        fetch_origins(1, row(origin_tags[1]))
        fetch_targets(1, row("g2_sc"))
        fetch_origins(2, row(origin_tags[0]))
        z0_turned = sb([P, HOPS // P, KP], BF16, "z0_turned")
        weigh_turned(0)
        z0 = [sb([P, HALF, PACK], BF16, "z0", tag=tag) for tag in ("got_w0", "g1")]
        for k in range(1, PACK):
            if k > 1:
                turn_rate(k)
            differ(k)
            weigh_turned(k)
            if k == PACK - 1:
                preweigh(LAST, f"rate0_{k}")
            place(k + 2)
            fetch_targets(k + 1, row("g2_sc"))
            if k < PACK - 1:
                fetch_origins(k + 2, row(origin_tags[k % 2]))
        both = row(origin_tags[1], 2 * HOPS)
        fetch_origins(5, both[:, 0:HOPS])
        fetch_targets(5, both[:, HOPS : 2 * HOPS])
        place(6)
        far, whole = row("g2_sc"), row(feats_tag(PACK - 1))
        fetch_targets(6, far[:, 0:HALF], 0, HALF)
        fetch_origins(6, whole[:, 0:HALF], 0, HALF)
        fetch_targets(6, far[:, HALF:HOPS], HALF, HOPS)
        for lo in range(HALF, HOPS, QUARTER):
            fetch_origins(6, whole[:, lo : lo + QUARTER], lo, lo + QUARTER)
        low = sb([P, 2, HOPS], F32, "low", tag="g2")
        differ(4)
        turn_back(0)
        differ(5)
        z1 = sb([P, HOPS, PACK], BF16, "z1", tag="raw512_0")
        for h, half in enumerate(halves):
            for k in (4, 5):
                turn_out(k, half.start, half.stop, low[:, k - PACK, :], low[:, k - PACK, :])
            nc.gpsimd.tensor_tensor(
                z1[:, half, 0:2].rearrange("p (c i) s -> p c s i", i=PACK),
                low[:, :, half].rearrange("p s (c i) -> p c s i", i=PACK),
                rate_low[:, :, half].rearrange("p s (c i) -> p c s i", i=PACK),
                ALU.mult,
            )
        turn_back(1)
        damps[6] = damp_tile(6)
        for lo in range(0, HOPS + QUARTER, QUARTER):
            if lo < HOPS:
                turn_in(6, lo, lo + QUARTER)
            if 0 < lo < HOPS:
                turn_out(6, lo - QUARTER, lo, ending, ending)
        turn_out(6, HOPS - QUARTER, HOPS, row("roots"), ending)
        place(LAST)

        def invert(part, diff):
            nc.scalar.activation(part, diff, ACT.Square)
            nc.scalar.activation(part, part, ACT.Square, bias=1.0)
            nc.scalar.activation(part, part, ACT.Abs_reciprocal_sqrt)

        quarters = ending[:].rearrange("p (q m) -> p q m", m=QUARTER)
        home = (8, 9, 10, 4)

        def slot3(lo, hi):
            return quarters[:, home[lo // QUARTER], lo % QUARTER : lo % QUARTER + hi - lo]

        def difference(lo, hi):
            start = max(s for kk, s in origins if kk == LAST and s <= lo)
            fetch_difference(LAST, origins[LAST, start][:, lo - start : hi - start], slot3(lo, hi), lo, hi)
            invert(slot3(lo, hi), slot3(lo, hi))

        def product(lo, hi):
            nc.vector.tensor_tensor(slot3(lo, hi), slot3(lo, hi), rate_last[:, lo:hi], ALU.mult)

        def weave(lo, hi):
            q = lo // QUARTER
            pair = quarters[:, q : home[q] + 1 : home[q] - q, lo % QUARTER : lo % QUARTER + hi - lo]
            nc.vector.tensor_copy(z1[:, lo:hi, 2:PACK], pair.rearrange("p s m -> p m s"))

        def pack(lo, hi):
            quantise_z(1, z1[:, lo:hi, :], lo, hi, sb([P, hi - lo], U32, f"codes1_{lo}")[:])

        first_pass(0, f"rate1_2_{HALF + QUARTER}")
        early = row("roots", HALF)
        fetch_origins(LAST, early[:, 0:QUARTER], 0, QUARTER)
        fetch_origins(LAST, row("got_w0", QUARTER), QUARTER, HALF)
        difference(0, 256)
        difference(256, 512)
        fetch_origins(LAST, early[:, 0:HALF], HALF, HOPS)
        first_pass(1, "got_w0")
        difference(512, 768)
        product(0, 256)
        product(256, 512)
        weave(0, 256)
        difference(768, 896)
        difference(896, 1024)
        pack(0, 256)
        weave(256, 512)
        product(512, 768)
        pack(256, 512)
        weave(512, 768)
        product(768, 896)
        product(896, 1024)
        pack(512, 768)
        weave(768, 896)
        weave(896, 1024)
        pack(768, 896)
        pack(896, 1024)
        for lo, hi in ((0, 128), (128, 256), (256, 512), (512, 640), (640, 768), (768, 896), (896, 1024)):
            score(lo, hi)
